import numpy as np, ml_dtypes
CORES = [2,6,10,14,18,22,26,30]
N = 8
import mx_ref
BF = ml_dtypes.bfloat16
def gentries(a):
    return np.ascontiguousarray(a.reshape(8, 16, -1).transpose(0, 2, 1)).reshape(8, -1)
def gtable(e):
    e = np.asarray(e); return np.ascontiguousarray(e.reshape(8, -1, 16).transpose(0, 2, 1)).reshape(128, -1).astype(np.int32)
def gcols(t, e):
    v = np.concatenate([t.reshape(8, 16, -1, 4), np.zeros((8, 16, 1, 4), BF)], axis=2)
    return np.ascontiguousarray(np.stack([v[g][:, e[g]] for g in range(8)])).reshape(128, -1)
def tile(rs):
    return np.stack(rs, axis=2).reshape(128, -1).astype(BF)
def pick(q, e):
    c = np.concatenate([q[0].reshape(128, -1, 4), np.zeros((128, 1, 4), np.uint8)], axis=1); s = np.concatenate([q[1], np.ones((16, 1), np.uint8)], axis=1)
    return (np.ascontiguousarray(c[:, e].reshape(128, -1)), np.ascontiguousarray(s[:, e]))
def join(*qs):
    return (np.concatenate([q[0] for q in qs], axis=1), np.concatenate([q[1] for q in qs], axis=1))
def put(q, e, v):
    c, s = q[0].reshape(128, -1, 4).copy(), q[1].copy(); c[:, e] = v[0].reshape(128, -1, 4); s[:, e] = v[1]
    return (c.reshape(128, -1), s)
def pk(c, s):
    return (np.ascontiguousarray(c), mx_ref.live(s))
def emit(q):
    return q[0], q[1]
def packed(v, rng):
    q = [mx_ref.quantize(np.ascontiguousarray(v[r])) for r in range(N)]
    return np.stack([a for a, b in q]), np.stack([mx_ref.plane(b, rng) for a, b in q])
def values_of_codes():
    e, c = np.zeros((128, 128, 4), np.float32), np.zeros((128, 2, 4), np.uint8)
    e[np.arange(128), np.arange(128), 0] = 1
    c[:127, :, 0] = np.arange(256).reshape(2, 128).T[:127]
    return mx_ref.matmul(mx_ref.quantize(e.reshape(128, 512).astype(BF)), (c.reshape(128, 8), np.full((16, 2), 127, np.uint8))).T.reshape(-1).astype(np.float64)
CODE_VALUE, SCALE_VALUE = values_of_codes(), 2.0 ** (np.arange(256) - 127.0)
def decode(q):
    return (CODE_VALUE[q[0]].reshape(16, 8, -1, 4) * SCALE_VALUE[q[1]][:, None, :, None] + 0.0).reshape(128, -1).astype(np.float32)
def f(rng, *shape):
    return mx_ref.flush((rng.standard_normal(shape, dtype=np.float32) * np.exp2(rng.integers(-2, 3, shape[:-1] + (1,)))).astype(BF))
def wide(rng, *shape, cols=0):
    v = rng.standard_normal(shape, dtype=np.float32) * np.exp2(rng.integers(-12, 13, shape)).astype(np.float32)
    if cols: v *= np.repeat(np.exp2(rng.integers(-cols, cols + 1, shape[:-2] + (1, shape[-1] // 4))) * (rng.random(shape[:-2] + (1, shape[-1] // 4)) > 0.0625), 4, axis=-1).astype(np.float32)
    return mx_ref.flush(v.astype(BF))
C, HALF, E = 256, 128, 192
MASK = [1, 2, 4]
TIMES = 8
def register(b):
    a = 2 * np.arange(HALF)
    return np.concatenate([a + b, a + 1 - b], axis=-1)
def lowest(s):
    low, to = np.broadcast_to(np.arange(C), s.shape), s
    for i in range(TIMES):
        low = np.minimum(low, np.take_along_axis(low, to, axis=-1))
        to = np.take_along_axis(to, to, axis=-1)
    return low
def joined(s):
    low, c = lowest(s), np.arange(HALF)
    a, b = low[..., :HALF], low[..., HALF:]
    swap = (a != b) & ((a == c) & (c > 0) | (b == c + HALF))
    return np.concatenate([np.where(swap, s[..., HALF:], s[..., :HALF]), np.where(swap, s[..., :HALF], s[..., HALF:])], axis=-1)
def numbers_of(rng):
    return {"x": np.array(f(rng, N, 128, 4 * C)), "u": np.array(f(rng, N, 128, 512)), "v": np.array(f(rng, N, 128, 512))}
def orders(rng):
    return rng.permuted(np.tile(np.arange(C), (N, 8, 1)), axis=2)
def stored(k):
    return {"kl": np.stack([gtable(k[r]) for r in range(N)])}
def layers(rng):
    return np.array(f(rng, N, 128, 2048)).reshape(N, 8, 16, 4, 8, 16, 4)
def weights(rng, w):
    c, p = packed(np.ascontiguousarray(w).reshape(N, 128, 2048), rng)
    return {"wc": c, "ws": p}
def setup_inputs(rng):
    return {**numbers_of(rng), **stored(orders(rng)), **weights(rng, layers(rng))}
def setup_inputs_ties(rng):
    d = numbers_of(rng)
    o = rng.permutation(N)
    k = rng.integers(-1, 2, (N, 8, C)).astype(np.float32)
    k[o[1]] = 1
    x = d["x"].reshape(N, 8, 16, C, 4)
    x[:, :, 0] = 0
    x[:, :, 0, :, 0] = k.astype(BF)
    a = np.exp2(rng.integers(-3, 4, (8, 1)).astype(np.float64))
    j = rng.integers(3, 7, (8, 4, 6))
    j[:, :, 0] = 6
    q = (9 + 2 * rng.integers(0, 4, (8, 4, 6))) * 0.125 * np.exp2(-j.astype(np.float64))
    x[:, :, 8:] = 0
    x[:, :, 8, :, 0] = (-3.0 * a).astype(np.float32).astype(BF)
    x[:, :, 10, :, 0] = (-0.140625 * a).astype(np.float32).astype(BF)
    x[:, :, 10, :, 1] = (-0.125 * a).astype(np.float32).astype(BF)
    c = np.ones(N, np.float32)
    c[o[0]] = 0
    c[o[2]] = -1
    u = d["u"].reshape(N, 128, 128, 4)
    u[:, :, ::16] = 0
    for h in range(0, 128, 16): u[:, h, h, 0] = c.astype(BF)
    w = layers(rng)
    w[:, :, 0] = 0
    w[:, :, :, :, :, 0] = 0
    w[:, :, :, :, :, 8:] = 0
    for g in range(8): w[:, g, 10, 0, g, 8, 0] = -224.0
    for n, i in enumerate((9, 11, 12, 13, 14, 15)):
        x[:, :, i] = (q[:, :, n] * a * -0.0078125)[:, None].astype(np.float32).astype(BF)
        for g in range(8): w[:, g, 10, :, g, i, 1] = (-q[g, :, n]).astype(np.float32).astype(BF)
    return {"x": x.reshape(N, 128, 4 * C), "u": u.reshape(N, 128, 512), "v": d["v"], **stored(orders(rng)), **weights(rng, w)}
def setup_inputs_near(rng):
    d = numbers_of(rng)
    o = rng.permutation(N) % 4
    k = np.where((o == 1) | (o == 2), 1.0, 2.0 ** -30).astype(np.float32)
    x = d["x"].astype(np.float32).reshape(N, 8, 16, C, 4)
    x[:, :, :8] = 0
    s = rng.integers(-1, 2, (N, 8, C)) * k[:, None, None]
    s[o == 3] = 0
    x[:, :, 0, :, 0] = 1.125 * s
    x[:, :, 1, :, 0] = -1.25 * s
    x[:, :, 7, :, 0] = 2.0 ** -30
    w = layers(rng)
    w[:, :, :8] = 0
    w[:, :, :, :, :, :8] = 0
    for r in range(N):
        if o[r] == 3:
            x[r, :, 4, :, 0] = rng.choice([-1.0, 1.0], (8, C)) * 2.0 ** -30
            for g in range(8):
                w[r, g, 4, 0, g, 0, 0] = 1.125 * 2.0 ** -8
                w[r, g, 4, 0, g, 1, 0] = -1.25 * 2.0 ** -8
                w[r, g, 7, 0, g, 6, 0] = 2.0 ** 5
        at = [0, C - 1, int(rng.integers(C)), int(rng.integers(C))]
        for g, j in zip(rng.permutation(8)[:4], at): x[r, g, 0, j, 0] = 2.0 ** 30 * rng.choice([-1.0, 1.0])
    u = d["u"].reshape(N, 128, 128, 4)
    u[:, :, ::16] = 0
    for h in range(0, 128, 16):
        u[:, h, h, 0] = (1.125 * k).astype(np.float32).astype(BF)
        u[:, h + 1, h, 0] = k.astype(BF)
    return {"x": x.reshape(N, 128, 4 * C).astype(BF), "u": u.reshape(N, 128, 512), "v": d["v"], **stored(orders(rng)), **weights(rng, w)}
def setup_inputs_long(rng):
    d = numbers_of(rng)
    k = orders(rng)
    b = rng.integers(0, 2, (N, 8, HALF))
    for c in rng.permutation(HALF):
        low = lowest(register(b))
        b[..., c] ^= (low[..., c] != low[..., c + HALF]).astype(np.int64)
    last = HALF - 1 - (HALF - 1) // 2
    way = [last >> i for i in range(last.bit_length() - 1, -1, -1)]
    for r in range(N):
        t = rng.permutation(8)
        for g in t[2:4]: b[r, g, rng.integers(1, HALF)] ^= 1
        b[r, t[4], 0] ^= 1
        for g in t[5:]: b[r, g] = rng.integers(0, 2, HALF)
        for g in t[5:7]:
            b[r, g, HALF - 1] = 0
            for i, j in zip(way, way[1:]): b[r, g, HALF - 1 - i] = j & 1
            b[r, g, HALF - 1 - last] = 1 - (HALF - 1) % 2
    s = np.zeros((N, 8, C))
    np.put_along_axis(s, k, np.concatenate([b, rng.integers(0, 2, (N, 8, HALF))], axis=2) * 2.0 - 1.0, axis=2)
    x = d["x"].reshape(N, 8, 16, C, 4)
    x[:, :, 0] = 0
    x[:, :, 0, :, 0] = (s * np.exp2(rng.integers(-3, 4, (N, 8, C)).astype(np.float64))).astype(np.float32).astype(BF)
    u = d["u"].reshape(N, 128, 128, 4)
    u[:, :, ::16] = 0
    for h in range(0, 128, 16): u[:, h, h, 0] = 1
    w = layers(rng)
    w[:, :, :, :, :, 0] = (w[:, :, :, :, :, 0].astype(np.float32) * 4).astype(BF)
    return {"x": x.reshape(N, 128, 4 * C), "u": u.reshape(N, 128, 512), "v": d["v"], **stored(k), **weights(rng, w)}
def setup_inputs_ends(rng):
    d = numbers_of(rng)
    o, e = rng.permutation(N) % 4, rng.permutation(N) % 4
    k = orders(rng)
    x = np.zeros((N, 8, 16, C, 4))
    u = d["u"].astype(np.float32).reshape(N, 128, 128, 4)
    v = np.zeros((N, 128, 512))
    w = np.zeros((N, 128, 4, 128, 4), np.float32)
    i = np.arange(128)[np.arange(128) % 16 < 15]
    j = np.arange(14, 128, 16)
    up, down = np.arange(C), np.arange(C)[::-1]
    for r in range(N):
        if e[r] == 0: k[r] = up
        if e[r] == 1: k[r] = down
        if e[r] == 2: k[r] = np.where(rng.permutation(8)[:, None] < 4, up, down)
        h = rng.permutation(8)
        c = np.where(h < 2, 0.0, h % 2 * 2.0 - 1.0)[None, :, None]
        much = (0.9 + 0.1 * rng.random((8, 16, C, 4))) * 2.0 ** 29
        if o[r] == 0: x[r] = -much
        if o[r] == 1: x[r] = much * rng.choice([-1.0, 1.0], (1, 1, C, 1))
        if o[r] == 2: x[r] = -(1.0 + 0.125 * rng.integers(0, 8, (8, 16, C, 4))) * 2.0 ** -30
        if o[r] == 3: x[r] = d["x"][r].astype(np.float32).reshape(8, 16, C, 4)[:, :, :1]
        x[r, :, 15] = 2.0 ** -30
        if o[r] < 2:
            u[r, :, ::16] = c * (0.9 + 0.1 * rng.random((128, 8, 4))) * 2.0 ** 30
            v[r] = (0.9 + 0.1 * rng.random((128, 512))) * 2.0 ** 30
        else:
            v[r] = (1.0 + 0.125 * rng.integers(0, 8, (128, 512))) * 2.0 ** -30
        if o[r] == 2: u[r, :, ::16] = c * (1.0 + 0.125 * rng.integers(0, 8, (128, 8, 4))) * 2.0 ** -30
        if o[r] == 3: u[r, :, ::16] *= np.abs(c).astype(np.float32)
        n = np.array([1.0, 2.0, 4.0])[rng.permutation(8) % 3]
        for b in range(4):
            if o[r] != 2: w[r, i, b, i, b] = -n[i // 16]
            else:
                w[r, i, b, i, b] = -2.0 ** -8
                w[r, j, b, j, b] = 0.0
                w[r, j + 1, b, j, b] = 2.0 ** 8
                w[r, j - 8, b, j - 8, b] = 0.0
                w[r, j + 1, b, j - 8, b] = 2.0 ** 5
    v = v * rng.choice([-1.0, 1.0], (N, 128, 512))
    return {"x": x.astype(np.float32).reshape(N, 128, 4 * C).astype(BF), "u": u.reshape(N, 128, 512).astype(BF), "v": v.astype(np.float32).astype(BF), **stored(k), **weights(rng, w.astype(BF))}
def setup_inputs_spread(rng):
    d = setup_inputs(rng)
    d["x"] = wide(rng, N, 128, 4 * C, cols=6)
    return d
def check_inputs(d):
    b = []
    for k in ("x", "u", "v"):
        a = np.abs(d[k].astype(np.float32))
        if not (np.isfinite(a).all() and ((a == 0) | (a >= 2.0 ** -30) & (a <= 2.0 ** 30)).all()): b.append("a value of " + k)
    none, least, most = [emit(mx_ref.quantize(np.full((128, 16), k, np.float32).astype(BF)))[1][0, 0] for k in (0.0, 2.0 ** -8, 2.0 ** 8)]
    for r in range(N):
        if not (np.sort(gentries(d["kl"][r]), axis=1) == np.arange(C)).all(): b.append("kl: not a permutation")
        if ((d["wc"][r] == 0x7F) | (d["wc"][r] == 0xFF)).any(): b.append("wc: a code that is no number")
        s = mx_ref.live(d["ws"][r])
        if ((s != none) & ((s < least) | (s > most))).any(): b.append("ws: a scale out of range")
    return b
def reference(x, u, v, kl, wc, ws):
    qu = [mx_ref.quantize(u[r]) for r in range(N)]
    lay = [pk(wc[r], ws[r]) for r in range(N)]
    now = [x[r] for r in range(N)]
    k = [gentries(kl[r]).astype(np.int64) for r in range(N)]
    for m in MASK:
        e, made = [], []
        for r in range(N):
            s = mx_ref.matmul(qu[r], mx_ref.quantize(now[r]))[::16]
            bits = (np.take_along_axis(s, k[r][:, :HALF], axis=1) > 0).astype(np.int64)
            e.append(np.take_along_axis(k[r], joined(register(bits)), axis=1))
            z = (gcols(now[r], k[r]).astype(np.float32) + gcols(now[r], e[r]).astype(np.float32)) * np.float32(0.5)
            q = mx_ref.quantize(z.astype(BF))
            made.append(tile([mx_ref.matmul(pick(lay[r], np.arange(128 * b, 128 * b + 128)), q) * np.float32(0.03125) for b in range(4)]))
        k = [np.take_along_axis(k[r ^ m], e[r], axis=1) for r in range(N)]
        for r in range(N):
            far = decode(mx_ref.quantize(np.ascontiguousarray(made[r ^ m][:, :4 * E]))).astype(BF)
            both = np.concatenate([far, made[r][:, 4 * E:]], axis=1)
            now[r] = (now[r].astype(np.float32) + gcols(both, k[r]).astype(np.float32)).astype(BF)
    y, kp = np.zeros((N, 128, C), np.float32), np.zeros((N, 8, C), np.float32)
    oc, osc = np.zeros((N, 128, 4 * C), np.uint8), np.zeros((N, 16, C), np.uint8)
    for r in range(N):
        q = mx_ref.quantize(now[r])
        y[r] = mx_ref.matmul(mx_ref.quantize(v[r]), q)
        kp[r] = k[r]
        oc[r], osc[r] = emit(q)
    return {"y": y, "kp": kp, "oc": oc, "osc": osc}

@@ -1,0 +1,395 @@
+from concourse.bass import DstId, RemoteDMATransfer
+from concourse.mybir import dt, AluOpType, ActivationFunctionType
+
+ROUNDS = 3
+LIFT = 512.0
+A = AluOpType
+CP = ActivationFunctionType.Copy
+
+SCRATCH = {
+    "ps": ("psum", [128, 4096], "float32"),
+    "kli": ("sbuf", [128, 16], "int32"),
+    "ut": ("sbuf", [128, 512], "bfloat16"),
+    "vt": ("sbuf", [128, 512], "bfloat16"),
+    "uq": ("sbuf", [128, 128], "float8_e4m3fn_x4"), "us": ("sbuf", [128, 128], "uint8"),
+    "up": ("sbuf", [128, 128], "float8_e4m3fn_x4"), "ups": ("sbuf", [128, 128], "uint8"),
+    "vq": ("sbuf", [128, 128], "float8_e4m3fn_x4"), "vqs": ("sbuf", [128, 128], "uint8"),
+    "wq": ("sbuf", [128, 512], "float8_e4m3fn_x4"), "wqs": ("sbuf", [128, 512], "uint8"),
+    "ones": ("sbuf", [128, 512], "bfloat16"),
+    "et": ("sbuf", [128, 2048], "bfloat16"),
+    "eq": ("sbuf", [128, 512], "float8_e4m3fn_x4"), "es": ("sbuf", [128, 512], "uint8"),
+    "pi": ("sbuf", [128, 4], "int32"),
+    "cs": ("sbuf", [128, 16], "float32"),
+    "i16": ("sbuf", [128, 256], "bfloat16"), "i4": ("sbuf", [128, 256], "bfloat16"),
+    "mt": ("sbuf", [128, 1024], "bfloat16"),
+    "m16": ("sbuf", [128, 256], "bfloat16"), "m4": ("sbuf", [128, 256], "bfloat16"),
+    "one": ("sbuf", [128, 256], "bfloat16"), "one2": ("sbuf", [128, 256], "bfloat16"),
+    "c21": ("sbuf", [128, 128], "bfloat16"), "c43": ("sbuf", [128, 128], "float32"),
+    "ci": ("sbuf", [128, 40], "float32"), "cc": ("sbuf", [128, 40], "float32"),
+    "cz": ("sbuf", [128, 40], "float32"), "cy": ("sbuf", [128, 40], "float32"),
+    "cmp": ("sbuf", [128, 40], "float32"), "c127": ("sbuf", [128, 8], "float32"),
+    "uo": ("sbuf", [128, 8], "uint16"),
+    "kyf": ("sbuf", [128, 256], "float32"),
+    "yo": ("sbuf", [128, 256], "float32"),
+    "x0": ("sbuf", [128, 1024], "bfloat16"),
+}
+for _r in range(ROUNDS + 1):
+    if _r:
+        SCRATCH["x%d" % _r] = ("sbuf", [128, 1024], "bfloat16")
+    SCRATCH["xq%d" % _r] = ("sbuf", [128, 256], "float8_e4m3fn_x4")
+    SCRATCH["xs%d" % _r] = ("sbuf", [128, 256], "uint8")
+for _r in range(ROUNDS):
+    for _n, _w, _d in (("xk", 1024, "bfloat16"), ("xj", 1024, "bfloat16"), ("lc", 8 * 256, "bfloat16"), ("z", 1024, "bfloat16"), ("h", 768, "bfloat16"), ("b", 1024, "bfloat16"),
+                       ("bit", 272, "bfloat16"), ("w", 8 * 256, "bfloat16"), ("low", 8 * 256, "bfloat16"),
+                       ("sc", 14 * 256, "bfloat16"), ("fr", 4 * 256, "bfloat16"), ("sm", 8 * 40, "float32"),
+                       ("to", 8 * 16, "uint16"), ("tt", 80, "uint16"),
+                       ("kf", 24, "float32"), ("k16_", 16, "uint16"), ("kb", 8, "uint16"), ("k4_", 64, "uint16"),
+                       ("kin", 16, "uint16")):
+        SCRATCH["%s%d" % (_n, _r)] = ("sbuf", [128, _w], _d)
+    for _n, _w in (("qz", 384), ("qh", 256), ("cin", 192)):
+        SCRATCH["%s_%d" % (_n, _r)] = ("sbuf", [128, _w], "float8_e4m3fn_x4")
+        SCRATCH["%ss_%d" % (_n, _r)] = ("sbuf", [128, _w], "uint8")
+SCRATCH["k4_3"] = ("sbuf", [128, 64], "uint16")
+
+SEMAPHORES = ["sv", "sa", "st", "sg", "dx", "du", "dk", "dwc", "dws", "dv", "dxk", "dout", "loc"]
+SEMAPHORES += ["%s%d" % (n, r) for r in range(ROUNDS) for n in ("rk", "ra", "rb")]
+
+
+def rank_program(g, core, T, topo):
+    rank = T.rank_of(core)
+    if rank is None:
+        return
+    queues = {"v": g.vector, "a": g.scalar, "t": g.tensor, "g": g, "y": g.sync}
+    own = {"v": "sv", "a": "sa", "t": "st", "g": "sg"}
+    done = {"sv": 0, "sa": 0, "st": 0, "sg": 0}
+    seen = {q: {} for q in queues}
+
+    def wait(q, *toks):
+        need = {}
+        for t in toks:
+            if t is not None:
+                need[t[0]] = max(need.get(t[0], 0), t[1])
+        for s, n in need.items():
+            if seen[q].get(s, 0) < n:
+                queues[q].wait_ge(T.sem[s], n)
+                seen[q][s] = n
+
+    def fin(q, ins):
+        s = own[q]
+        ins.then_inc(T.sem[s], 1)
+        done[s] += 1
+        return (s, done[s])
+
+    def dma(q, sem, total, out, in_):
+        queues[q].dma_start(out, in_).then_inc(T.sem[sem], 16)
+        return (sem, total)
+
+    def ts(out, in0, s1, s2, op0, op1, *toks):
+        wait("v", *toks)
+        if op1 is None:
+            return fin("v", g.vector.tensor_scalar(out, in0, s1, None, op0))
+        return fin("v", g.vector.tensor_scalar(out, in0, s1, s2, op0, op1))
+
+    def tt(out, in0, in1, op, *toks):
+        wait("v", *toks)
+        return fin("v", g.vector.tensor_tensor(out, in0, in1, op))
+
+    def vcopy(out, in_, *toks):
+        wait("v", *toks)
+        return fin("v", g.vector.tensor_copy(out, in_))
+
+    def scan(out, mask, data, *toks):
+        wait("v", *toks)
+        return fin("v", g.vector.tensor_tensor_scan(out, mask, data, 0.0, A.mult, A.max))
+
+    def quant(codes, plane, tile, *toks):
+        wait("v", *toks)
+        return fin("v", g.vector.quantize_mx(codes, plane, tile))
+
+    def act(out, in_, scale, *toks):
+        wait("a", *toks)
+        if scale is None:
+            return fin("a", g.scalar.activation(out, in_, CP))
+        return fin("a", g.scalar.activation(out, in_, CP, scale=scale))
+
+    def mm(bank, n, lq, ls, rq, rs, *toks):
+        wait("t", *toks)
+        return fin("t", g.tensor.matmul_mx(T.ps[:, 512 * bank:512 * bank + n], lq, ls, rq, rs, True, True))
+
+    def psv(bank, a, b):
+        return T.ps[:, 512 * bank + a:512 * bank + b]
+
+    def remote(r, out, in_, sem):
+        dst = T.cores[rank ^ (1 << r)]
+        rid, pid, _ = topo.addr(dst)
+        ne = len(topo.engines(core, dst))
+        g.remote_dma(out, in_, T.sem[sem], T.sem.loc, pid, rid, topo.mask(core, dst))
+        loc[0] += ne
+        return ne
+
+    loc = [0]
+    cs = T.cs
+
+    t_kl = dma("y", "dk", 16, T.kli[:], T.kl[:])
+    t_x = dma("y", "dx", 16, T.x0[:], T.x[:])
+    t_u = dma("a", "du", 16, T.ut[:], T.u[:])
+    t_wc = dma("y", "dwc", 16, T.wq[:, 0:512].bitcast(dt.uint8), T.wc[:])
+    t_ws = dma("y", "dws", 16, T.wqs[:], T.ws[:])
+    t_v = dma("y", "dv", 16, T.vt[:], T.v[:])
+
+    def iota(out, pat, base, ch, small=True):
+        if small:
+            return fin("g", g.iota(out, pat, base, ch, allow_small_or_imprecise_dtypes=True))
+        return fin("g", g.iota(out, pat, base, ch))
+    g_pi = iota(T.pi[:, 0:1], [[0, 1]], 0, 1, False)
+    g_ci = iota(T.ci[:, 32:40], [[16, 8]], 0, 0)
+    g_one = iota(T.one[:], [[1, 256]], 1, 0)
+    g_i4 = iota(T.i4[:], [[0, 64], [1, 4]], 0, 0)
+    g_i16 = iota(T.i16[:], [[0, 16], [1, 16]], 0, 0)
+    g_c21 = iota(T.c21[:], [[2, 128]], 1, 0)
+    g_c43 = iota(T.c43[:], [[4, 128]], 3, 0)
+    g_ci4 = iota(T.ci[:, 0:32], [[4, 32]], 0, 0)
+
+    v_ones = fin("v", g.vector.memset(T.ones[:], 1.0))
+    v_bit = None
+    for r in range(ROUNDS):
+        v_bit = fin("v", g.vector.memset(T["bit%d" % r][:, 256:272], 1.0))
+    ts(T.pi[:, 1:2], T.pi[:, 0:1], 15, None, A.bitwise_and, None, g_pi)
+    ts(T.pi[:, 2:3], T.pi[:, 0:1], 2, 3, A.logical_shift_right, A.bitwise_and)
+    t = ts(T.pi[:, 3:4], T.pi[:, 0:1], 3, None, A.bitwise_and, None)
+    v_uo = vcopy(T.uo[:], T.ci[:, 32:40], g_ci)
+    t = vcopy(cs[:, 0:3], T.pi[:, 1:4], t)
+    q_, r_ = cs[:, 0:1], cs[:, 1:2]
+    ts(cs[:, 3:4], cs[:, 2:3], 4.0, None, A.subtract, None, t)
+    ts(cs[:, 8:9], q_, 15.0, 1.0 - 1.0 / LIFT, A.is_equal, A.mult)
+    ts(cs[:, 9:10], r_, 3.0, 4.0 - 4.0 / LIFT, A.is_equal, A.mult)
+    ts(cs[:, 10:11], q_, 15.0, 1.0 - LIFT, A.is_equal, A.mult)
+    t = ts(cs[:, 11:12], r_, 3.0, 1.0 - LIFT, A.is_equal, A.mult)
+    ts(cs[:, 4:5], cs[:, 8:9], 1.0 / LIFT, None, A.add, None, t)
+    ts(cs[:, 5:6], cs[:, 9:10], 4.0 / LIFT, None, A.add, None)
+    ts(cs[:, 6:7], cs[:, 10:11], LIFT, None, A.add, None)
+    v_cs = ts(cs[:, 7:8], cs[:, 11:12], LIFT, None, A.add, None)
+    un16, un4, tau4 = cs[:, 4:5], cs[:, 5:6], cs[:, 3:4]
+
+    v_kf = vcopy(T.kf0[:, 0:16], T.kli[:], t_kl)
+    v_k16 = vcopy(T.k16_0[:], T.kli[:])
+    v_kfr = vcopy(T.fr0[:, 0:256], T.one[:].indirect(T.k16_0[:, 0:16]), v_k16, g_one)
+
+    v_one2 = vcopy(T.one2[:], T.one[:])
+    mt = T.mt
+    ts(mt[:, 0:256], T.i4[:], r_, 0.0, A.subtract, A.is_gt, g_i4)
+    ta = ts(mt[:, 256:512], T.i4[:], r_, 1.0, A.subtract, A.is_equal)
+    ts(mt[:, 512:768], T.i16[:], q_, 0.0, A.subtract, A.is_gt, g_i16)
+    tb = ts(mt[:, 768:1024], T.i16[:], q_, 1.0, A.subtract, A.is_equal)
+    ta = ts(T.m4[:], mt[:, 256:512], LIFT, None, A.mult, None, ta)
+    tb = ts(T.m16[:], mt[:, 768:1024], LIFT, None, A.mult, None, tb)
+    ta = tt(mt[:, 256:512], mt[:, 0:256], T.m4[:], A.max, ta)
+    tb = tt(mt[:, 768:1024], mt[:, 512:768], T.m16[:], A.max, tb)
+    m4, m16 = mt[:, 256:512], mt[:, 768:1024]
+    v_m4, v_m16 = ta, tb
+    t = scan(T.sc0[:, 13 * 256:14 * 256], m4, T.fr0[:, 0:256], v_kfr, v_m4, v_m16)
+    v_k4 = ts(T.k4_0[:], T.sc0[:, 13 * 256 + 3:14 * 256:4], un4, tau4, A.mult, A.add, t, v_cs)
+
+    v_q1 = quant(T.xq0[:, 0:128], T.xs0[:, 0:128], T.x0[:, 0:512], t_x)
+    v_q2 = quant(T.xq0[:, 128:256], T.xs0[:, 128:256], T.x0[:, 512:1024])
+    t = quant(T.uq[:, 0:128], T.us[:, 0:128], T.ut[:, 0:512], t_u)
+    vcopy(T.up[:, 0:128].bitcast(dt.uint32), T.uq[:, 0:128].bitcast(dt.uint32).indirect(T.uo[:, 0:8]), t, v_uo)
+    v_up = vcopy(T.ups[:, 0:128], T.us[:, 0:128].indirect(T.uo[:, 0:8]))
+
+    ts(T.cc[:, 0:32], T.ci[:, 0:32], r_, None, A.add, None, g_ci4)
+    t = ts(T.cc[:, 32:40], T.ci[:, 32:40], q_, None, A.add, None)
+    v_c127 = ts(T.c127[:], T.cc[:, 32:40], 127.0, 256.0, A.is_equal, A.mult, t)
+    t = ts(T.cz[:], T.cc[:], 0.0, -2.0, A.is_equal, A.mult)
+    t = tt(T.cy[:], T.cc[:], T.cz[:], A.add, t)
+    ts(T.cmp[:, 0:32], T.cy[:, 0:32], 1.0, cs[:, 7:8], A.add, A.mult, t)
+    v_cmp = ts(T.cmp[:, 32:40], T.cy[:, 32:40], 1.0, cs[:, 6:7], A.add, A.mult)
+    t = tt(T.kf0[:, 16:24], T.kf0[:, 0:8], T.c127[:], A.max, v_c127)
+    v_kb = vcopy(T.kb0[:], T.kf0[:, 16:24], t)
+
+    wait("g", v_k16)
+    rk = [remote(0, T.kin0[:], T.k16_0[:], "rk0"), 0, 0]
+    g_e = []
+    wait("g", v_ones)
+    for b in range(4):
+        g_e.append(fin("g", g.affine_select(T.et[:, 512 * b:512 * b + 512], T.ones[:], [[-1, 512]], A.is_equal, 0.0, b, 4)))
+
+    bankuse = [[] for _ in range(8)]
+    x_done = (t_x,)
+    for r in range(ROUNDS):
+        X, xk, Z, H, B = T["x%d" % r], T["xk%d" % r], T["z%d" % r], T["h%d" % r], T["b%d" % r]
+        xq, xs, bit, W, low, SC = T["xq%d" % r], T["xs%d" % r], T["bit%d" % r], T["w%d" % r], T["low%d" % r], T["sc%d" % r]
+        fr, sm, to, tw = T["fr%d" % r], T["sm%d" % r], T["to%d" % r], T["tt%d" % r]
+        last = r == ROUNDS - 1
+
+        def sc(i):
+            return SC[:, 256 * i:256 * i + 256]
+
+        a_xk = act(xk[:], X[:].indirect(T["k4_%d" % r][:, 0:64]), 0.5, v_k4, *x_done)
+        xk2 = T["xj%d" % r]
+        wait("y", a_xk)
+        d_xk = dma("y", "dxk", 16 * (r + 1), xk2[:], xk[:])
+
+        sb = (4, 5)
+        p1 = mm(sb[0], 128, T.up[:, 0:128], T.ups[:, 0:128], xq[:, 0:128], xs[:, 0:128], v_q1, v_up, *bankuse[sb[0]])
+        p2 = mm(sb[1], 128, T.up[:, 0:128], T.ups[:, 0:128], xq[:, 128:256], xs[:, 128:256], v_q2, *bankuse[sb[1]])
+        ts(bit[:, 0:128], psv(sb[0], 0, 128), 0.0, None, A.is_gt, None, p1)
+        t = ts(bit[:, 128:256], psv(sb[1], 0, 128), 0.0, None, A.is_gt, None, p2)
+        bankuse[sb[0]], bankuse[sb[1]] = [t], [t]
+        tl = tt(W[:, 0:128], bit[:, 0:272].indirect(T["kb%d" % r][:, 0:8]), T.c21[:], A.add, t, v_kb, v_bit, g_c21)
+        th = tt(W[:, 128:256], T.c43[:], W[:, 0:128], A.subtract, tl, g_c43)
+        scan(SC[:, 0:128], mt[:, 768:896], W[:, 0:128], tl)
+        t = scan(SC[:, 128:256], mt[:, 768:896], W[:, 128:256], th)
+        v_to = ts(to[:, 0:16], SC[:, 15:256:16], un16, 1.0, A.mult, A.subtract, t)
+
+        lowv, lowc, v_low, v_lc, a_w, t16w = T.one[:], T.one2[:], None, v_one2, th, None
+        for k in range(8):
+            nl = low[:, 256 * k:256 * k + 256]
+            off = to[:, 16 * k:16 * k + 16]
+            if k < 7:
+                a_w = act(W[:, 256 * k + 256:256 * k + 512], W[:, 256 * k:256 * k + 256].indirect(off), None, v_to, a_w)
+            v_low = tt(nl, lowv.indirect(off), lowc, A.min, v_to, v_low, v_lc)
+            lowv, lowc = nl, T["lc%d" % r][:, 256 * k:256 * k + 256]
+            if k == 0:
+                t4 = scan(sc(9), m4, W[:, 0:256])
+                ts(sm[:, 32:40], SC[:, 15:128:16], un16, 1.0, A.mult, A.subtract)
+                ts(sm[:, 72:80], SC[:, 143:256:16], un16, 1.0, A.mult, A.subtract)
+            if k == 1:
+                ts(sm[:, 0:32], SC[:, 9 * 256 + 3:9 * 256 + 128:4], un4, tau4, A.mult, A.add, t4)
+                t16w = ts(sm[:, 40:72], SC[:, 9 * 256 + 131:10 * 256:4], un4, tau4, A.mult, A.add)
+            if k == 2:
+                tt(sm[:, 80:120], sm[:, 40:80], sm[:, 0:40], A.subtract, t16w)
+            if k < 7:
+                t = scan(sc(k + 1), m16, W[:, 256 * k + 256:256 * k + 512], a_w)
+                v_lc = vcopy(lowc, lowv, v_low)
+                v_to = ts(to[:, 16 * k + 16:16 * k + 32], SC[:, 256 * (k + 1) + 15:256 * (k + 2):16], un16, 1.0, A.mult, A.subtract, t)
+        t4 = scan(sc(10), m4, lowv, v_low)
+        t16 = scan(sc(11), m16, lowv)
+        e1 = tt(sm[:, 120:152], SC[:, 10 * 256 + 3:10 * 256 + 128:4], T.cmp[:, 0:32], A.is_equal, t4, v_cmp)
+        tt(sm[:, 160:192], SC[:, 10 * 256 + 131:11 * 256:4], T.cmp[:, 0:32], A.not_equal)
+        e1 = tt(sm[:, 152:160], SC[:, 11 * 256 + 15:11 * 256 + 128:16], T.cmp[:, 32:40], A.is_equal, t16)
+        e2 = tt(sm[:, 192:200], SC[:, 11 * 256 + 143:12 * 256:16], T.cmp[:, 32:40], A.not_equal)
+        t = tt(sm[:, 200:240], sm[:, 120:160], sm[:, 80:120], A.mult, e1)
+        t = tt(sm[:, 240:280], sm[:, 200:240], sm[:, 160:200], A.mult, t, e2)
+        tlo = tt(sm[:, 280:320], sm[:, 0:40], sm[:, 240:280], A.add, t)
+        thi = tt(sm[:, 200:240], sm[:, 40:80], sm[:, 240:280], A.subtract)
+        clo = vcopy(tw[:, 0:40], sm[:, 280:320], tlo)
+        chi = vcopy(tw[:, 40:80], sm[:, 200:240], thi)
+
+        ne = rk[r]
+        f1 = act(fr[:, 256:512], T.one[:].indirect(T["kin%d" % r][:, 0:16]), None, ("rk%d" % r, ne), g_one)
+        f2 = act(fr[:, 512:768], fr[:, 256:512].indirect(T["k16_%d" % r][:, 0:16]), None, f1, v_k16)
+        act(fr[:, 768:896], fr[:, 512:768].indirect(tw[:, 32:40]), None, f2, clo)
+        a_n = act(fr[:, 896:1024], fr[:, 512:768].indirect(tw[:, 72:80]), None, chi)
+
+        def layer(qz, qzs, banks, tok):
+            out = []
+            for b in range(4):
+                out.append(mm(banks[b], 128, T.wq[:, 128 * b:128 * b + 128], T.wqs[:, 128 * b:128 * b + 128], qz, qzs,
+                              tok, t_wc, t_ws, *bankuse[banks[b]]))
+            return out
+
+        def nm(s):
+            return T["%s_%d" % (s, r)]
+        z1 = tt(Z[:, 0:512], xk[:].indirect(tw[:, 0:32]), xk2[:, 0:512], A.add, clo, a_xk, d_xk)
+        tq = quant(nm("qz")[:, 0:128], nm("qzs")[:, 0:128], Z[:, 0:512], z1)
+        p = layer(nm("qz")[:, 0:128], nm("qzs")[:, 0:128], (0, 1, 2, 3), tq)
+        h1 = []
+        for b in range(4):
+            h1.append(act(H[:, b:512:4], psv(b, 0, 128), 0.03125, p[b]))
+            bankuse[b] = [h1[b]]
+        z2 = tt(Z[:, 512:768], xk[:].indirect(tw[:, 40:56]), xk2[:, 512:768], A.add, chi)
+        tq = quant(nm("qz")[:, 128:256], nm("qzs")[:, 128:256], Z[:, 256:768], z2)
+        p = layer(nm("qz")[:, 128:256], nm("qzs")[:, 128:256], (4, 5, 6, 7), tq)
+        tq1 = quant(nm("qh")[:, 0:128], nm("qhs")[:, 0:128], H[:, 0:512], h1[3])
+        h2 = [None] * 4
+        for b in (0, 2):
+            h2[b] = ts(H[:, 512 + b:768:4], psv(4 + b, 64, 128), 0.03125, None, A.mult, None, p[b])
+            bankuse[4 + b] = [h2[b]]
+        for b in (1, 3):
+            h2[b] = act(H[:, 512 + b:768:4], psv(4 + b, 64, 128), 0.03125, p[b])
+            bankuse[4 + b] = [h2[b]]
+        tq2 = quant(nm("qh")[:, 128:256], nm("qhs")[:, 128:256], H[:, 256:768], h2[2], h2[3])
+
+        wait("g", tq1)
+        na = remote(r, nm("cin")[:, 0:128].bitcast(dt.uint8), nm("qh")[:, 0:128].bitcast(dt.uint8), "ra%d" % r)
+        na += remote(r, nm("cins")[:, 0:128], nm("qhs")[:, 0:128], "ra%d" % r)
+        wait("g", tq2)
+        nb = remote(r, nm("cin")[:, 128:192].bitcast(dt.uint8), nm("qh")[:, 192:256].bitcast(dt.uint8), "rb%d" % r)
+        nb += remote(r, nm("cins")[:, 128:192], nm("qhs")[:, 192:256], "rb%d" % r)
+
+        z3 = tt(Z[:, 768:1024], xk[:].indirect(tw[:, 56:72]), xk2[:, 768:1024], A.add)
+        s16 = None
+        if not last:
+            s16 = scan(sc(12), m16, fr[:, 768:1024], a_n)
+        s4 = scan(sc(13) if r else sc(9), m4, fr[:, 768:1024], a_n)
+        tq = quant(nm("qz")[:, 256:384], nm("qzs")[:, 256:384], Z[:, 512:1024], z3)
+        p = layer(nm("qz")[:, 256:384], nm("qzs")[:, 256:384], (0, 1, 2, 3), tq)
+        for b in range(4):
+            t = act(B[:, 768 + b:1024:4], psv(b, 64, 128), 0.03125, p[b])
+            bankuse[b] = [t]
+        a_b = t
+        s4o = 256 * (13 if r else 9)
+        if not last:
+            kf = T["kf%d" % (r + 1)]
+            v_k16 = ts(T["k16_%d" % (r + 1)][:], SC[:, 12 * 256 + 15:13 * 256:16], un16, 1.0, A.mult, A.subtract, s16)
+            v_kf = ts(kf[:, 0:16], SC[:, 12 * 256 + 15:13 * 256:16], un16, 1.0, A.mult, A.subtract)
+            v_k4 = ts(T["k4_%d" % (r + 1)][:], SC[:, s4o + 3:s4o + 256:4], un4, tau4, A.mult, A.add, s4)
+            t = tt(kf[:, 16:24], kf[:, 0:8], T.c127[:], A.max, v_kf)
+            v_kb = vcopy(T["kb%d" % (r + 1)][:], kf[:, 16:24], t)
+            wait("g", v_k16)
+            rk[r + 1] = remote(r + 1, T["kin%d" % (r + 1)][:], T["k16_%d" % (r + 1)][:], "rk%d" % (r + 1))
+        else:
+            v_k4 = ts(T["k4_%d" % (r + 1)][:], SC[:, s4o + 3:s4o + 256:4], un4, tau4, A.mult, A.add, s4)
+            v_ky = ts(T.kyf[:], fr[:, 768:1024], 1.0, None, A.subtract, None)
+        if r == 0:
+            for b in range(4):
+                v_e = quant(T.eq[:, 128 * b:128 * b + 128], T.es[:, 128 * b:128 * b + 128], T.et[:, 512 * b:512 * b + 512], g_e[b])
+            v_v = quant(T.vq[:, 0:128], T.vqs[:, 0:128], T.vt[:], t_v)
+
+        cin, cins = nm("cin"), nm("cins")
+        p = []
+        for b in range(4):
+            p.append(mm(4 + b, 128, T.eq[:, 128 * b:128 * b + 128], T.es[:, 128 * b:128 * b + 128], cin[:, 0:128], cins[:, 0:128],
+                        ("ra%d" % r, na), v_e, *bankuse[4 + b]))
+        for b in range(4):
+            t = act(B[:, b:512:4], psv(4 + b, 0, 128), None, p[b])
+            bankuse[4 + b] = [t]
+        p = []
+        for b in range(4):
+            p.append(mm(b, 128, T.eq[:, 128 * b:128 * b + 128], T.es[:, 128 * b:128 * b + 128], cin[:, 64:192], cins[:, 64:192],
+                        ("rb%d" % r, nb), *bankuse[b]))
+        bt = []
+        for b in range(4):
+            o, i = B[:, 512 + b:768:4], psv(b, 64, 128)
+            t = vcopy(o, i, p[b]) if b % 2 == 0 else act(o, i, None, p[b])
+            bankuse[b] = [t]
+            bt.append(t)
+
+        nx, n4 = T["x%d" % (r + 1)], T["k4_%d" % (r + 1)]
+        nq, ns = T["xq%d" % (r + 1)], T["xs%d" % (r + 1)]
+        g1 = tt(nx[:, 0:512], B[:].indirect(n4[:, 0:32]), X[:, 0:512], A.add, v_k4, a_b, *bt)
+        g2 = tt(nx[:, 512:1024], B[:].indirect(n4[:, 32:64]), X[:, 512:1024], A.add)
+        v_q1 = quant(nq[:, 0:128], ns[:, 0:128], nx[:, 0:512], g1)
+        v_q2 = quant(nq[:, 128:256], ns[:, 128:256], nx[:, 512:1024], g2)
+        x_done = (g1, g2)
+
+    nd = [0]
+
+    def out(q, o, i, *toks):
+        wait(q, *toks)
+        queues[q].dma_start(o, i).then_inc(T.sem.dout, 16)
+        nd[0] += 16
+    xq, xs = T["xq%d" % ROUNDS], T["xs%d" % ROUNDS]
+    p1 = mm(4, 128, T.vq[:, 0:128], T.vqs[:, 0:128], xq[:, 0:128], xs[:, 0:128], v_q1, v_v, *bankuse[4])
+    p2 = mm(5, 128, T.vq[:, 0:128], T.vqs[:, 0:128], xq[:, 128:256], xs[:, 128:256], v_q2, *bankuse[5])
+    y1 = vcopy(T.yo[:, 0:128], psv(4, 0, 128), p1)
+    y2 = vcopy(T.yo[:, 128:256], psv(5, 0, 128), p2)
+    out("y", T.kp[:], T.kyf[0:128:16, :], v_ky)
+    out("y", T.oc[:], xq[:, 0:256].bitcast(dt.uint8), v_q2)
+    out("a", T.osc[0:4, :], xs[0:4, :], v_q2)
+    out("y", T.osc[4:8, :], xs[32:36, :])
+    out("a", T.osc[8:12, :], xs[64:68, :])
+    out("y", T.osc[12:16, :], xs[96:100, :])
+    out("a", T.y[:], T.yo[:], y1, y2)
+
+    wait("g", ("dout", nd[0]), ("loc", loc[0]), *[(s, n) for s, n in done.items()])

@@ -20,14 +20,14 @@ SCRATCH = {
     "eq": ("sbuf", [128, 512], "float8_e4m3fn_x4"), "es": ("sbuf", [128, 512], "uint8"),
     "pi": ("sbuf", [128, 4], "int32"),
     "cs": ("sbuf", [128, 16], "float32"),
-    "i16": ("sbuf", [128, 256], "bfloat16"), "i4": ("sbuf", [128, 256], "bfloat16"),
-    "mt": ("sbuf", [128, 1024], "bfloat16"),
-    "m16": ("sbuf", [128, 256], "bfloat16"), "m4": ("sbuf", [128, 256], "bfloat16"),
+    "i16": ("sbuf", [128, 16], "float32"), "ms": ("sbuf", [128, 64], "bfloat16"), "mw": ("sbuf", [128, 32], "bfloat16"),
+    "oq": ("sbuf", [128, 16], "uint16"), "ot": ("sbuf", [128, 16], "uint16"),
+    "mt": ("sbuf", [128, 512], "bfloat16"),
+    "d0": ("sbuf", [128, 160], "float32"), "d1": ("sbuf", [128, 160], "float32"),
     "one": ("sbuf", [128, 256], "bfloat16"), "one2": ("sbuf", [128, 256], "bfloat16"),
     "c21": ("sbuf", [128, 128], "bfloat16"), "c43": ("sbuf", [128, 128], "float32"),
-    "ci": ("sbuf", [128, 40], "float32"), "cc": ("sbuf", [128, 40], "float32"),
-    "cz": ("sbuf", [128, 40], "float32"), "cy": ("sbuf", [128, 40], "float32"),
-    "cmp": ("sbuf", [128, 40], "float32"), "c127": ("sbuf", [128, 8], "float32"),
+    "ci": ("sbuf", [128, 40], "float32"), "cc": ("sbuf", [128, 160], "float32"),
+    "c127": ("sbuf", [128, 8], "float32"),
     "uo": ("sbuf", [128, 8], "uint16"),
     "kyf": ("sbuf", [128, 256], "float32"),
     "yo": ("sbuf", [128, 256], "float32"),
@@ -41,7 +41,7 @@ for _r in range(ROUNDS + 1):
 for _r in range(ROUNDS):
     for _n, _w, _d in (("xk", 1024, "bfloat16"), ("xj", 1024, "bfloat16"), ("lc", 8 * 256, "bfloat16"), ("z", 1024, "bfloat16"), ("h", 768, "bfloat16"), ("b", 1024, "bfloat16"),
                        ("bit", 272, "bfloat16"), ("w", 8 * 256, "bfloat16"), ("low", 8 * 256, "bfloat16"),
-                       ("sc", 14 * 256, "bfloat16"), ("fr", 4 * 256, "bfloat16"), ("sm", 8 * 40, "float32"),
+                       ("sc", 14 * 256, "bfloat16"), ("fr", 4 * 256, "bfloat16"), ("sm", 40, "float32"), ("so", 160, "float32"),
                        ("to", 8 * 16, "uint16"), ("tt", 80, "uint16"),
                        ("kf", 24, "float32"), ("k16_", 16, "uint16"), ("kb", 8, "uint16"), ("k4_", 64, "uint16"),
                        ("kin", 16, "uint16")):
@@ -102,6 +102,10 @@ def rank_program(g, core, T, topo):
         wait("v", *toks)
         return fin("v", g.vector.tensor_tensor_scan(out, mask, data, 0.0, A.mult, A.max))
 
+    def chain(out, mul, add, *toks):
+        wait("v", *toks)
+        return fin("v", g.vector.tensor_tensor_scan(out, mul, add, 0.0, A.mult, A.add))
+
     def quant(codes, plane, tile, *toks):
         wait("v", *toks)
         return fin("v", g.vector.quantize_mx(codes, plane, tile))
@@ -128,7 +132,7 @@ def rank_program(g, core, T, topo):
         return ne
 
     loc = [0]
-    cs = T.cs
+    cs, d0, d1 = T.cs, T.d0, T.d1
 
     t_kl = dma("y", "dk", 16, T.kli[:], T.kl[:])
     t_x = dma("y", "dx", 16, T.x0[:], T.x[:])
@@ -142,25 +146,40 @@ def rank_program(g, core, T, topo):
             return fin("g", g.iota(out, pat, base, ch, allow_small_or_imprecise_dtypes=True))
         return fin("g", g.iota(out, pat, base, ch))
     g_pi = iota(T.pi[:, 0:1], [[0, 1]], 0, 1, False)
+    g_is = iota(T.i16[:], [[1, 16]], 0, 0)
     g_ci = iota(T.ci[:, 32:40], [[16, 8]], 0, 0)
+    g_ci4 = iota(T.ci[:, 0:32], [[4, 32]], 0, 0)
     g_one = iota(T.one[:], [[1, 256]], 1, 0)
-    g_i4 = iota(T.i4[:], [[0, 64], [1, 4]], 0, 0)
-    g_i16 = iota(T.i16[:], [[0, 16], [1, 16]], 0, 0)
     g_c21 = iota(T.c21[:], [[2, 128]], 1, 0)
     g_c43 = iota(T.c43[:], [[4, 128]], 3, 0)
-    g_ci4 = iota(T.ci[:, 0:32], [[4, 32]], 0, 0)
 
-    v_ones = fin("v", g.vector.memset(T.ones[:], 1.0))
+    t = fin("v", g.vector.memset(T.d0[:], -1.0))
     v_bit = None
     for r in range(ROUNDS):
         v_bit = fin("v", g.vector.memset(T["bit%d" % r][:, 256:272], 1.0))
+    ts(T.d0[:, 0:160:4], T.d0[:, 0:160:4], 0.0, None, A.mult, None, t)
     ts(T.pi[:, 1:2], T.pi[:, 0:1], 15, None, A.bitwise_and, None, g_pi)
     ts(T.pi[:, 2:3], T.pi[:, 0:1], 2, 3, A.logical_shift_right, A.bitwise_and)
     t = ts(T.pi[:, 3:4], T.pi[:, 0:1], 3, None, A.bitwise_and, None)
     v_uo = vcopy(T.uo[:], T.ci[:, 32:40], g_ci)
     t = vcopy(cs[:, 0:3], T.pi[:, 1:4], t)
     q_, r_ = cs[:, 0:1], cs[:, 1:2]
-    ts(cs[:, 3:4], cs[:, 2:3], 4.0, None, A.subtract, None, t)
+    ms, mw = T.ms, T.mw
+    ts(ms[:, 16:32], T.i16[:], q_, 1.0, A.subtract, A.is_equal, g_is, t)
+    ta = ts(ms[:, 36:40], T.i16[:, 0:4], r_, 1.0, A.subtract, A.is_equal)
+    ts(ms[:, 0:16], T.i16[:], q_, 0.0, A.subtract, A.is_gt)
+    ts(ms[:, 32:36], T.i16[:, 0:4], r_, 0.0, A.subtract, A.is_gt)
+    ts(ms[:, 40:56], ms[:, 16:32], LIFT, None, A.mult, None, ta)
+    tb = ts(ms[:, 56:60], ms[:, 36:40], LIFT, None, A.mult, None)
+    ts(T.oq[:], T.i16[:], 0.0, q_, A.mult, A.add)
+    ts(T.ot[:], T.i16[:], 0.0, cs[:, 2:3], A.mult, A.add)
+    tt(mw[:, 0:16], ms[:, 0:16], ms[:, 40:56], A.max, tb)
+    t = tt(mw[:, 16:20], ms[:, 32:36], ms[:, 56:60], A.max)
+    m16, m4 = T.mt[:, 0:256], T.mt[:, 256:512]
+    act(m16, mw[:, 0:16].indirect(T.oq[:]), None, t)
+    a_m = act(m4, mw[:, 16:20].indirect(T.ot[:]), None)
+
+    ts(cs[:, 3:4], cs[:, 2:3], 4.0, None, A.subtract, None)
     ts(cs[:, 8:9], q_, 15.0, 1.0 - 1.0 / LIFT, A.is_equal, A.mult)
     ts(cs[:, 9:10], r_, 3.0, 4.0 - 4.0 / LIFT, A.is_equal, A.mult)
     ts(cs[:, 10:11], q_, 15.0, 1.0 - LIFT, A.is_equal, A.mult)
@@ -171,45 +190,45 @@ def rank_program(g, core, T, topo):
     v_cs = ts(cs[:, 7:8], cs[:, 11:12], LIFT, None, A.add, None)
     un16, un4, tau4 = cs[:, 4:5], cs[:, 5:6], cs[:, 3:4]
 
-    v_kf = vcopy(T.kf0[:, 0:16], T.kli[:], t_kl)
-    v_k16 = vcopy(T.k16_0[:], T.kli[:])
-    v_kfr = vcopy(T.fr0[:, 0:256], T.one[:].indirect(T.k16_0[:, 0:16]), v_k16, g_one)
+    cc = T.cc
+    ts(cc[:, 0:32], T.ci[:, 0:32], r_, None, A.add, None, g_ci4)
+    v_cc = ts(cc[:, 32:40], T.ci[:, 32:40], q_, None, A.add, None)
+    v_one2 = vcopy(T.one2[:], T.one[:], g_one)
+    v_c127 = ts(T.c127[:], cc[:, 32:40], 127.0, 256.0, A.is_equal, A.mult, v_cc)
 
-    v_one2 = vcopy(T.one2[:], T.one[:])
-    mt = T.mt
-    ts(mt[:, 0:256], T.i4[:], r_, 0.0, A.subtract, A.is_gt, g_i4)
-    ta = ts(mt[:, 256:512], T.i4[:], r_, 1.0, A.subtract, A.is_equal)
-    ts(mt[:, 512:768], T.i16[:], q_, 0.0, A.subtract, A.is_gt, g_i16)
-    tb = ts(mt[:, 768:1024], T.i16[:], q_, 1.0, A.subtract, A.is_equal)
-    ta = ts(T.m4[:], mt[:, 256:512], LIFT, None, A.mult, None, ta)
-    tb = ts(T.m16[:], mt[:, 768:1024], LIFT, None, A.mult, None, tb)
-    ta = tt(mt[:, 256:512], mt[:, 0:256], T.m4[:], A.max, ta)
-    tb = tt(mt[:, 768:1024], mt[:, 512:768], T.m16[:], A.max, tb)
-    m4, m16 = mt[:, 256:512], mt[:, 768:1024]
-    v_m4, v_m16 = ta, tb
-    t = scan(T.sc0[:, 13 * 256:14 * 256], m4, T.fr0[:, 0:256], v_kfr, v_m4, v_m16)
-    v_k4 = ts(T.k4_0[:], T.sc0[:, 13 * 256 + 3:14 * 256:4], un4, tau4, A.mult, A.add, t, v_cs)
+    def tables(k):
+        if k == 0:
+            ts(cs[:, 12:13], tau4, 2.0, 12.0, A.mult, A.add, v_cs)
+        if k == 1:
+            ts(cc[:, 40:80], cc[:, 0:40], 0.0, -2.0, A.is_equal, A.mult)
+        if k == 2:
+            ts(d1[:, 131:160:4], cc[:, 32:40], 4.0, 1.0, A.mult, A.add)
+            ts(d1[:, 3:128:4], cc[:, 0:32], 16.0, cs[:, 12:13], A.mult, A.add)
+        if k == 3:
+            tt(cc[:, 80:120], cc[:, 0:40], cc[:, 40:80], A.add)
+        if k == 5:
+            ts(cc[:, 120:152], cc[:, 80:112], 1.0, cs[:, 7:8], A.add, A.mult)
+            ts(cc[:, 152:160], cc[:, 112:120], 1.0, cs[:, 6:7], A.add, A.mult)
+    cmp4, cmp16 = cc[:, 120:152], cc[:, 152:160]
 
+    v_k16 = vcopy(T.k16_0[:], T.kli[:], t_kl)
+    v_kf = vcopy(T.kf0[:, 0:16], T.kli[:])
+    a_kfr = act(T.fr0[:, 0:256], T.one[:].indirect(T.k16_0[:, 0:16]), None, v_k16, g_one)
+
+    v_uq = quant(T.uq[:, 0:128], T.us[:, 0:128], T.ut[:, 0:512], t_u)
     v_q1 = quant(T.xq0[:, 0:128], T.xs0[:, 0:128], T.x0[:, 0:512], t_x)
+    v_up = vcopy(T.up[:, 0:128].bitcast(dt.uint32), T.uq[:, 0:128].bitcast(dt.uint32).indirect(T.uo[:, 0:8]), v_uq, v_uo)
+    a_up = act(T.ups[:, 0:128], T.us[:, 0:128].indirect(T.uo[:, 0:8]), None, v_uq, v_uo)
     v_q2 = quant(T.xq0[:, 128:256], T.xs0[:, 128:256], T.x0[:, 512:1024])
-    t = quant(T.uq[:, 0:128], T.us[:, 0:128], T.ut[:, 0:512], t_u)
-    vcopy(T.up[:, 0:128].bitcast(dt.uint32), T.uq[:, 0:128].bitcast(dt.uint32).indirect(T.uo[:, 0:8]), t, v_uo)
-    v_up = vcopy(T.ups[:, 0:128], T.us[:, 0:128].indirect(T.uo[:, 0:8]))
-
-    ts(T.cc[:, 0:32], T.ci[:, 0:32], r_, None, A.add, None, g_ci4)
-    t = ts(T.cc[:, 32:40], T.ci[:, 32:40], q_, None, A.add, None)
-    v_c127 = ts(T.c127[:], T.cc[:, 32:40], 127.0, 256.0, A.is_equal, A.mult, t)
-    t = ts(T.cz[:], T.cc[:], 0.0, -2.0, A.is_equal, A.mult)
-    t = tt(T.cy[:], T.cc[:], T.cz[:], A.add, t)
-    ts(T.cmp[:, 0:32], T.cy[:, 0:32], 1.0, cs[:, 7:8], A.add, A.mult, t)
-    v_cmp = ts(T.cmp[:, 32:40], T.cy[:, 32:40], 1.0, cs[:, 6:7], A.add, A.mult)
-    t = tt(T.kf0[:, 16:24], T.kf0[:, 0:8], T.c127[:], A.max, v_c127)
-    v_kb = vcopy(T.kb0[:], T.kf0[:, 16:24], t)
+    tk = tt(T.kf0[:, 16:24], T.kf0[:, 0:8], T.c127[:], A.max, v_kf, v_c127)
+    t = scan(T.sc0[:, 13 * 256:14 * 256], m4, T.fr0[:, 0:256], a_kfr, a_m)
+    v_kb = vcopy(T.kb0[:], T.kf0[:, 16:24], tk)
+    v_k4 = ts(T.k4_0[:], T.sc0[:, 13 * 256 + 3:14 * 256:4], un4, tau4, A.mult, A.add, t, v_cs)
 
     wait("g", v_k16)
     rk = [remote(0, T.kin0[:], T.k16_0[:], "rk0"), 0, 0]
     g_e = []
-    wait("g", v_ones)
+    wait("g", iota(T.ones[:], [[0, 512]], 1, 0))
     for b in range(4):
         g_e.append(fin("g", g.affine_select(T.et[:, 512 * b:512 * b + 512], T.ones[:], [[-1, 512]], A.is_equal, 0.0, b, 4)))
 
@@ -230,15 +249,15 @@ def rank_program(g, core, T, topo):
         d_xk = dma("y", "dxk", 16 * (r + 1), xk2[:], xk[:])
 
         sb = (4, 5)
-        p1 = mm(sb[0], 128, T.up[:, 0:128], T.ups[:, 0:128], xq[:, 0:128], xs[:, 0:128], v_q1, v_up, *bankuse[sb[0]])
+        p1 = mm(sb[0], 128, T.up[:, 0:128], T.ups[:, 0:128], xq[:, 0:128], xs[:, 0:128], v_q1, v_up, a_up, *bankuse[sb[0]])
         p2 = mm(sb[1], 128, T.up[:, 0:128], T.ups[:, 0:128], xq[:, 128:256], xs[:, 128:256], v_q2, *bankuse[sb[1]])
         ts(bit[:, 0:128], psv(sb[0], 0, 128), 0.0, None, A.is_gt, None, p1)
         t = ts(bit[:, 128:256], psv(sb[1], 0, 128), 0.0, None, A.is_gt, None, p2)
         bankuse[sb[0]], bankuse[sb[1]] = [t], [t]
         tl = tt(W[:, 0:128], bit[:, 0:272].indirect(T["kb%d" % r][:, 0:8]), T.c21[:], A.add, t, v_kb, v_bit, g_c21)
         th = tt(W[:, 128:256], T.c43[:], W[:, 0:128], A.subtract, tl, g_c43)
-        scan(SC[:, 0:128], mt[:, 768:896], W[:, 0:128], tl)
-        t = scan(SC[:, 128:256], mt[:, 768:896], W[:, 128:256], th)
+        scan(SC[:, 0:128], m16[:, 0:128], W[:, 0:128], tl)
+        t = scan(SC[:, 128:256], m16[:, 0:128], W[:, 128:256], th)
         v_to = ts(to[:, 0:16], SC[:, 15:256:16], un16, 1.0, A.mult, A.subtract, t)
 
         lowv, lowc, v_low, v_lc, a_w, t16w = T.one[:], T.one2[:], None, v_one2, th, None
@@ -249,37 +268,39 @@ def rank_program(g, core, T, topo):
                 a_w = act(W[:, 256 * k + 256:256 * k + 512], W[:, 256 * k:256 * k + 256].indirect(off), None, v_to, a_w)
             v_low = tt(nl, lowv.indirect(off), lowc, A.min, v_to, v_low, v_lc)
             lowv, lowc = nl, T["lc%d" % r][:, 256 * k:256 * k + 256]
-            if k == 0:
-                t4 = scan(sc(9), m4, W[:, 0:256])
-                ts(sm[:, 32:40], SC[:, 15:128:16], un16, 1.0, A.mult, A.subtract)
-                ts(sm[:, 72:80], SC[:, 143:256:16], un16, 1.0, A.mult, A.subtract)
-            if k == 1:
-                ts(sm[:, 0:32], SC[:, 9 * 256 + 3:9 * 256 + 128:4], un4, tau4, A.mult, A.add, t4)
-                t16w = ts(sm[:, 40:72], SC[:, 9 * 256 + 131:10 * 256:4], un4, tau4, A.mult, A.add)
-            if k == 2:
-                tt(sm[:, 80:120], sm[:, 40:80], sm[:, 0:40], A.subtract, t16w)
             if k < 7:
+                v_lc = act(lowc, lowv, None, v_low)
                 t = scan(sc(k + 1), m16, W[:, 256 * k + 256:256 * k + 512], a_w)
-                v_lc = vcopy(lowc, lowv, v_low)
+                if r == 0:
+                    tables(k)
+                if k == 0:
+                    t4 = scan(SC[:, 9 * 256:9 * 256 + 128], m4[:, 0:128], W[:, 0:128])
+                if k == 1:
+                    ts(d1[:, 2:128:4], SC[:, 9 * 256 + 3:9 * 256 + 128:4], un4, tau4, A.mult, A.add, t4)
+                if k == 2:
+                    td = ts(d1[:, 130:160:4], SC[:, 15:128:16], un16, 1.0, A.mult, A.subtract)
+                if k == 3:
+                    td = ts(sm[:, 0:40], d1[:, 2:160:4], -2.0, None, A.mult, None, td)
+                if k == 4:
+                    v_d = tt(d0[:, 2:160:4], sm[:, 0:40], d1[:, 3:160:4], A.add, td)
                 v_to = ts(to[:, 16 * k + 16:16 * k + 32], SC[:, 256 * (k + 1) + 15:256 * (k + 2):16], un16, 1.0, A.mult, A.subtract, t)
+        so = T["so%d" % r]
         t4 = scan(sc(10), m4, lowv, v_low)
         t16 = scan(sc(11), m16, lowv)
-        e1 = tt(sm[:, 120:152], SC[:, 10 * 256 + 3:10 * 256 + 128:4], T.cmp[:, 0:32], A.is_equal, t4, v_cmp)
-        tt(sm[:, 160:192], SC[:, 10 * 256 + 131:11 * 256:4], T.cmp[:, 0:32], A.not_equal)
-        e1 = tt(sm[:, 152:160], SC[:, 11 * 256 + 15:11 * 256 + 128:16], T.cmp[:, 32:40], A.is_equal, t16)
-        e2 = tt(sm[:, 192:200], SC[:, 11 * 256 + 143:12 * 256:16], T.cmp[:, 32:40], A.not_equal)
-        t = tt(sm[:, 200:240], sm[:, 120:160], sm[:, 80:120], A.mult, e1)
-        t = tt(sm[:, 240:280], sm[:, 200:240], sm[:, 160:200], A.mult, t, e2)
-        tlo = tt(sm[:, 280:320], sm[:, 0:40], sm[:, 240:280], A.add, t)
-        thi = tt(sm[:, 200:240], sm[:, 40:80], sm[:, 240:280], A.subtract)
-        clo = vcopy(tw[:, 0:40], sm[:, 280:320], tlo)
-        chi = vcopy(tw[:, 40:80], sm[:, 200:240], thi)
+        tt(d1[:, 0:128:4], SC[:, 10 * 256 + 131:11 * 256:4], cmp4, A.is_equal, t4)
+        e4 = tt(d1[:, 1:128:4], SC[:, 10 * 256 + 3:10 * 256 + 128:4], cmp4, A.is_equal)
+        tt(d1[:, 128:160:4], SC[:, 11 * 256 + 143:12 * 256:16], cmp16, A.is_equal, t16)
+        e16 = tt(d1[:, 129:160:4], SC[:, 11 * 256 + 15:11 * 256 + 128:16], cmp16, A.is_equal)
+        s4 = chain(so[:, 0:128], d0[:, 0:128], d1[:, 0:128], e4, v_d)
+        s16 = chain(so[:, 128:160], d0[:, 128:160], d1[:, 128:160], e16)
+        clo = vcopy(tw[:, 0:32], so[:, 2:128:4], s4)
+        chi = vcopy(tw[:, 40:72], so[:, 3:128:4])
+        c16 = vcopy(tw[:, 32:40], so[:, 130:160:4], s16)
 
         ne = rk[r]
         f1 = act(fr[:, 256:512], T.one[:].indirect(T["kin%d" % r][:, 0:16]), None, ("rk%d" % r, ne), g_one)
         f2 = act(fr[:, 512:768], fr[:, 256:512].indirect(T["k16_%d" % r][:, 0:16]), None, f1, v_k16)
-        act(fr[:, 768:896], fr[:, 512:768].indirect(tw[:, 32:40]), None, f2, clo)
-        a_n = act(fr[:, 896:1024], fr[:, 512:768].indirect(tw[:, 72:80]), None, chi)
+        act(fr[:, 768:896], fr[:, 512:768].indirect(tw[:, 32:40]), None, f2, c16)
 
         def layer(qz, qzs, banks, tok):
             out = []
@@ -291,6 +312,8 @@ def rank_program(g, core, T, topo):
         def nm(s):
             return T["%s_%d" % (s, r)]
         z1 = tt(Z[:, 0:512], xk[:].indirect(tw[:, 0:32]), xk2[:, 0:512], A.add, clo, a_xk, d_xk)
+        chi16 = vcopy(tw[:, 72:80], so[:, 131:160:4])
+        a_n = act(fr[:, 896:1024], fr[:, 512:768].indirect(tw[:, 72:80]), None, chi16)
         tq = quant(nm("qz")[:, 0:128], nm("qzs")[:, 0:128], Z[:, 0:512], z1)
         p = layer(nm("qz")[:, 0:128], nm("qzs")[:, 0:128], (0, 1, 2, 3), tq)
         h1 = []

@@ -3,6 +3,8 @@ from concourse.mybir import dt, AluOpType, ActivationFunctionType
 
 ROUNDS = 3
 LIFT = 512.0
+SINGLE = False
+SHARE = 32
 A = AluOpType
 CP = ActivationFunctionType.Copy
 
@@ -18,16 +20,16 @@ SCRATCH = {
     "ones": ("sbuf", [128, 512], "bfloat16"),
     "et": ("sbuf", [128, 2048], "bfloat16"),
     "eq": ("sbuf", [128, 512], "float8_e4m3fn_x4"), "es": ("sbuf", [128, 512], "uint8"),
-    "pi": ("sbuf", [128, 4], "int32"),
-    "cs": ("sbuf", [128, 16], "float32"),
+    "pi": ("sbuf", [128, 8], "int32"),
+    "cs": ("sbuf", [128, 24], "float32"),
     "i16": ("sbuf", [128, 16], "float32"), "ms": ("sbuf", [128, 64], "bfloat16"), "mw": ("sbuf", [128, 32], "bfloat16"),
     "oq": ("sbuf", [128, 16], "uint16"), "ot": ("sbuf", [128, 16], "uint16"),
     "mt": ("sbuf", [128, 512], "bfloat16"),
     "d0": ("sbuf", [128, 160], "float32"), "d1": ("sbuf", [128, 160], "float32"),
-    "one": ("sbuf", [128, 256], "bfloat16"), "one2": ("sbuf", [128, 256], "bfloat16"),
+    "one": ("sbuf", [128, 256], "bfloat16"),
     "c21": ("sbuf", [128, 128], "bfloat16"), "c43": ("sbuf", [128, 128], "float32"),
-    "ci": ("sbuf", [128, 40], "float32"), "cc": ("sbuf", [128, 160], "float32"),
-    "c127": ("sbuf", [128, 8], "float32"),
+    "ci": ("sbuf", [128, 40], "float32"), "cc": ("sbuf", [128, 120], "float32"),
+    "cmp": ("sbuf", [128, 80], "float32"), "c127": ("sbuf", [128, 24], "float32"), "mk": ("sbuf", [128, 448], "bfloat16"),
     "uo": ("sbuf", [128, 8], "uint16"),
     "kyf": ("sbuf", [128, 256], "float32"),
     "yo": ("sbuf", [128, 256], "float32"),
@@ -41,7 +43,7 @@ for _r in range(ROUNDS + 1):
 for _r in range(ROUNDS):
     for _n, _w, _d in (("xk", 1024, "bfloat16"), ("xj", 1024, "bfloat16"), ("lc", 8 * 256, "bfloat16"), ("z", 1024, "bfloat16"), ("h", 768, "bfloat16"), ("b", 1024, "bfloat16"),
                        ("bit", 272, "bfloat16"), ("w", 8 * 256, "bfloat16"), ("low", 8 * 256, "bfloat16"),
-                       ("sc", 14 * 256, "bfloat16"), ("fr", 4 * 256, "bfloat16"), ("sm", 40, "float32"), ("so", 160, "float32"),
+                       ("sc", 14 * 256, "bfloat16"), ("fr", 4 * 256, "bfloat16"), ("sm", 48, "float32"), ("so", 160, "float32"),
                        ("to", 8 * 16, "uint16"), ("tt", 80, "uint16"),
                        ("kf", 24, "float32"), ("k16_", 16, "uint16"), ("kb", 8, "uint16"), ("k4_", 64, "uint16"),
                        ("kin", 16, "uint16")):
@@ -152,18 +154,36 @@ def rank_program(g, core, T, topo):
     g_one = iota(T.one[:], [[1, 256]], 1, 0)
     g_c21 = iota(T.c21[:], [[2, 128]], 1, 0)
     g_c43 = iota(T.c43[:], [[4, 128]], 3, 0)
+    g_i2 = iota(T.mk[:, 0:64], [[0, 32], [1, 2]], 0, 0)
+    g_i8 = iota(T.mk[:, 64:128], [[0, 8], [1, 8]], 0, 0)
+    a_pre = [None] * ROUNDS
 
-    t = fin("v", g.vector.memset(T.d0[:], -1.0))
-    v_bit = None
-    for r in range(ROUNDS):
-        v_bit = fin("v", g.vector.memset(T["bit%d" % r][:, 256:272], 1.0))
-    ts(T.d0[:, 0:160:4], T.d0[:, 0:160:4], 0.0, None, A.mult, None, t)
+    def prefill(r):
+        act(T["low%d" % r][:, 0:128], T.one[:, 0:128], None, g_one)
+        a_pre[r] = act(T["lc%d" % r][:, 0:128], T.one[:, 0:128], None)
+
+    v_bit = fin("v", g.vector.memset(T.bit0[:, 256:272], 1.0))
     ts(T.pi[:, 1:2], T.pi[:, 0:1], 15, None, A.bitwise_and, None, g_pi)
     ts(T.pi[:, 2:3], T.pi[:, 0:1], 2, 3, A.logical_shift_right, A.bitwise_and)
+    ts(T.pi[:, 4:5], T.pi[:, 0:1], 1, 7, A.logical_shift_right, A.bitwise_and)
     t = ts(T.pi[:, 3:4], T.pi[:, 0:1], 3, None, A.bitwise_and, None)
     v_uo = vcopy(T.uo[:], T.ci[:, 32:40], g_ci)
-    t = vcopy(cs[:, 0:3], T.pi[:, 1:4], t)
+    vcopy(cs[:, 15:16], T.pi[:, 4:5], t)
+    t = vcopy(cs[:, 0:3], T.pi[:, 1:4])
     q_, r_ = cs[:, 0:1], cs[:, 1:2]
+
+    def fun(f, out, in_, scale, bias, *toks):
+        wait("a", *toks)
+        return fin("a", g.scalar.activation(out, in_, f, bias=bias, scale=scale))
+    ID, SG = ActivationFunctionType.Identity, ActivationFunctionType.Sign
+    fun(SG, cs[:, 8:9], q_, 1.0, -14.5, t)
+    a_cs = fun(SG, cs[:, 20:21], r_, 1.0, -2.5)
+    h = LIFT / 2
+    fun(ID, cs[:, 4:5], cs[:, 8:9], 0.5 - 0.5 / LIFT, 0.5 + 0.5 / LIFT, a_cs)
+    fun(ID, cs[:, 5:6], cs[:, 20:21], 2.0 - 2.0 / LIFT, 2.0 + 2.0 / LIFT)
+    fun(ID, cs[:, 6:7], cs[:, 8:9], 0.5 - h, 0.5 + h)
+    a_cs = fun(ID, cs[:, 7:8], cs[:, 20:21], 0.5 - h, 0.5 + h)
+    prefill(0)
     ms, mw = T.ms, T.mw
     ts(ms[:, 16:32], T.i16[:], q_, 1.0, A.subtract, A.is_equal, g_is, t)
     ta = ts(ms[:, 36:40], T.i16[:, 0:4], r_, 1.0, A.subtract, A.is_equal)
@@ -179,50 +199,64 @@ def rank_program(g, core, T, topo):
     act(m16, mw[:, 0:16].indirect(T.oq[:]), None, t)
     a_m = act(m4, mw[:, 16:20].indirect(T.ot[:]), None)
 
-    ts(cs[:, 3:4], cs[:, 2:3], 4.0, None, A.subtract, None)
-    ts(cs[:, 8:9], q_, 15.0, 1.0 - 1.0 / LIFT, A.is_equal, A.mult)
-    ts(cs[:, 9:10], r_, 3.0, 4.0 - 4.0 / LIFT, A.is_equal, A.mult)
-    ts(cs[:, 10:11], q_, 15.0, 1.0 - LIFT, A.is_equal, A.mult)
-    t = ts(cs[:, 11:12], r_, 3.0, 1.0 - LIFT, A.is_equal, A.mult)
-    ts(cs[:, 4:5], cs[:, 8:9], 1.0 / LIFT, None, A.add, None, t)
-    ts(cs[:, 5:6], cs[:, 9:10], 4.0 / LIFT, None, A.add, None)
-    ts(cs[:, 6:7], cs[:, 10:11], LIFT, None, A.add, None)
-    v_cs = ts(cs[:, 7:8], cs[:, 11:12], LIFT, None, A.add, None)
+    v_t4 = ts(cs[:, 3:4], cs[:, 2:3], 4.0, None, A.subtract, None)
+    v_cs = a_cs
     un16, un4, tau4 = cs[:, 4:5], cs[:, 5:6], cs[:, 3:4]
 
     cc = T.cc
-    ts(cc[:, 0:32], T.ci[:, 0:32], r_, None, A.add, None, g_ci4)
     v_cc = ts(cc[:, 32:40], T.ci[:, 32:40], q_, None, A.add, None)
-    v_one2 = vcopy(T.one2[:], T.one[:], g_one)
-    v_c127 = ts(T.c127[:], cc[:, 32:40], 127.0, 256.0, A.is_equal, A.mult, v_cc)
+    t = ts(T.c127[:, 8:16], cc[:, 32:40], 4.0, 3.0, A.mult, A.add, v_cc)
+    v_c127 = ts(T.c127[:, 0:8], cc[:, 32:40], 127.0, 256.0, A.is_equal, A.mult)
+    v_hic = ts(T.c127[:, 16:24], T.c127[:, 8:16], cs[:, 6:7], None, A.mult, None, t, a_cs)
 
     def tables(k):
-        if k == 0:
-            ts(cs[:, 12:13], tau4, 2.0, 12.0, A.mult, A.add, v_cs)
+        h = LIFT / 2
         if k == 1:
-            ts(cc[:, 40:80], cc[:, 0:40], 0.0, -2.0, A.is_equal, A.mult)
+            tab[1] = fun(ID, cs[:, 12:13], tau4, 2.0, 12.0, v_t4)
+            fin("v", g.vector.memset(d0[:], -1.0))
+            tab["bit"] = [None] + [fin("v", g.vector.memset(T["bit%d" % i][:, 256:272], 1.0)) for i in (1, 2)]
         if k == 2:
-            ts(d1[:, 131:160:4], cc[:, 32:40], 4.0, 1.0, A.mult, A.add)
-            ts(d1[:, 3:128:4], cc[:, 0:32], 16.0, cs[:, 12:13], A.mult, A.add)
+            fun(ID, cs[:, 13:14], cs[:, 18:19], 0.5 - h, 0.5 + h, tab[1])
+            fun(ID, cs[:, 14:15], cs[:, 19:20], 0.5 - h, 0.5 + h)
+            tab["sg"] = fun(SG, cc[:, 40:80], cc[:, 0:40], 1.0, -0.5, v_c127)
+            ts(d0[:, 0:160:4], d0[:, 0:160:4], 0.0, None, A.mult, None)
+            fun(ID, cs[:, 11:12], cs[:, 18:19], -h, h)
+            fun(SG, mk[:, 256:320], mk[:, 64:128], 1.0, cs[:, 16:17], g_i8)
+            tab[2] = fun(ActivationFunctionType.Abs, mk[:, 320:384], mk[:, 64:128], 1.0, cs[:, 17:18])
         if k == 3:
-            tt(cc[:, 80:120], cc[:, 0:40], cc[:, 40:80], A.add)
+            fun(ID, d1[:, 3:128:4], cc[:, 0:32], 16.0, cs[:, 12:13], tab[2])
+            fun(ID, d1[:, 131:160:4], cc[:, 32:40], 4.0, 1.0)
+            fun(ActivationFunctionType.Relu, mk[:, 384:448], mk[:, 320:384], -LIFT, LIFT)
+            tab[3] = fun(ID, mk[:, 128:192], mk[:, 0:64], cs[:, 11:12], 0.0, g_i2)
+            tab["cy"] = tt(cc[:, 80:120], cc[:, 0:40], cc[:, 40:80], A.add, tab["sg"])
         if k == 5:
-            ts(cc[:, 120:152], cc[:, 80:112], 1.0, cs[:, 7:8], A.add, A.mult)
-            ts(cc[:, 152:160], cc[:, 112:120], 1.0, cs[:, 6:7], A.add, A.mult)
-    cmp4, cmp16 = cc[:, 120:152], cc[:, 152:160]
+            fun(ID, cmp_[:, 0:32], cc[:, 80:112], cs[:, 7:8], 0.0, tab["cy"])
+            fun(ID, cmp_[:, 32:40], cc[:, 112:120], cs[:, 6:7], 0.0)
+            fun(ID, cmp_[:, 40:72], cc[:, 80:112], cs[:, 13:14], 0.0)
+            tab[5] = fun(ID, cmp_[:, 72:80], cc[:, 112:120], cs[:, 14:15], 0.0)
+            tab["m8"] = tt(mk[:, 192:256], mk[:, 256:320], mk[:, 384:448], A.max, tab[3])
+    tab = {}
+
+    cmp_, mk, hic = T.cmp, T.mk, T.c127[:, 16:24]
+    m2, m8 = mk[:, 128:192], mk[:, 192:256]
 
     v_k16 = vcopy(T.k16_0[:], T.kli[:], t_kl)
     v_kf = vcopy(T.kf0[:, 0:16], T.kli[:])
-    a_kfr = act(T.fr0[:, 0:256], T.one[:].indirect(T.k16_0[:, 0:16]), None, v_k16, g_one)
 
     v_uq = quant(T.uq[:, 0:128], T.us[:, 0:128], T.ut[:, 0:512], t_u)
-    v_q1 = quant(T.xq0[:, 0:128], T.xs0[:, 0:128], T.x0[:, 0:512], t_x)
+    tk = tt(T.kf0[:, 16:24], T.kf0[:, 0:8], T.c127[:, 0:8], A.max, v_kf, v_c127)
     v_up = vcopy(T.up[:, 0:128].bitcast(dt.uint32), T.uq[:, 0:128].bitcast(dt.uint32).indirect(T.uo[:, 0:8]), v_uq, v_uo)
-    a_up = act(T.ups[:, 0:128], T.us[:, 0:128].indirect(T.uo[:, 0:8]), None, v_uq, v_uo)
-    v_q2 = quant(T.xq0[:, 128:256], T.xs0[:, 128:256], T.x0[:, 512:1024])
-    tk = tt(T.kf0[:, 16:24], T.kf0[:, 0:8], T.c127[:], A.max, v_kf, v_c127)
-    t = scan(T.sc0[:, 13 * 256:14 * 256], m4, T.fr0[:, 0:256], a_kfr, a_m)
     v_kb = vcopy(T.kb0[:], T.kf0[:, 16:24], tk)
+    v_q1 = quant(T.xq0[:, 0:128], T.xs0[:, 0:128], T.x0[:, 0:512], t_x)
+    a_up = act(T.ups[:, 0:128], T.us[:, 0:128].indirect(T.uo[:, 0:8]), None, v_uq, v_uo)
+    a_kfr = act(T.fr0[:, 0:256], T.one[:].indirect(T.k16_0[:, 0:16]), None, v_k16, g_one)
+    fun(SG, cs[:, 18:19], r_, 1.0, -1.5)
+    fun(SG, cs[:, 19:20], q_, 1.0, -13.5)
+    fun(ID, cc[:, 0:32], T.ci[:, 0:32], 1.0, r_, g_ci4)
+    fun(ID, cs[:, 16:17], cs[:, 15:16], -1.0, 0.0)
+    fun(ID, cs[:, 17:18], cs[:, 15:16], -1.0, -1.0)
+    v_q2 = quant(T.xq0[:, 128:256], T.xs0[:, 128:256], T.x0[:, 512:1024])
+    t = scan(T.sc0[:, 13 * 256:14 * 256], m4, T.fr0[:, 0:256], a_kfr, a_m)
     v_k4 = ts(T.k4_0[:], T.sc0[:, 13 * 256 + 3:14 * 256:4], un4, tau4, A.mult, A.add, t, v_cs)
 
     wait("g", v_k16)
@@ -254,43 +288,62 @@ def rank_program(g, core, T, topo):
         ts(bit[:, 0:128], psv(sb[0], 0, 128), 0.0, None, A.is_gt, None, p1)
         t = ts(bit[:, 128:256], psv(sb[1], 0, 128), 0.0, None, A.is_gt, None, p2)
         bankuse[sb[0]], bankuse[sb[1]] = [t], [t]
-        tl = tt(W[:, 0:128], bit[:, 0:272].indirect(T["kb%d" % r][:, 0:8]), T.c21[:], A.add, t, v_kb, v_bit, g_c21)
-        th = tt(W[:, 128:256], T.c43[:], W[:, 0:128], A.subtract, tl, g_c43)
-        scan(SC[:, 0:128], m16[:, 0:128], W[:, 0:128], tl)
-        t = scan(SC[:, 128:256], m16[:, 0:128], W[:, 128:256], th)
-        v_to = ts(to[:, 0:16], SC[:, 15:256:16], un16, 1.0, A.mult, A.subtract, t)
+        tl = tt(W[:, 0:128], bit[:, 0:272].indirect(T["kb%d" % r][:, 0:8]), T.c21[:], A.add, t, v_kb, tab["bit"][r] if r else v_bit, g_c21)
+        t = scan(SC[:, 0:128], m16[:, 0:128], W[:, 0:128], tl)
+        th = tt(W[:, 128:256], T.c43[:], W[:, 0:128], A.subtract, g_c43)
+        t = tt(sm[:, 40:48], hic, SC[:, 15:128:16], A.subtract, t, v_hic)
+        v_tl = ts(to[:, 0:8], SC[:, 15:128:16], un16, 1.0, A.mult, A.subtract)
+        v_to = ts(to[:, 8:16], sm[:, 40:48], un16, 1.0, A.mult, A.subtract, t)
 
-        lowv, lowc, v_low, v_lc, a_w, t16w = T.one[:], T.one2[:], None, v_one2, th, None
-        for k in range(8):
-            nl = low[:, 256 * k:256 * k + 256]
-            off = to[:, 16 * k:16 * k + 16]
-            if k < 7:
-                a_w = act(W[:, 256 * k + 256:256 * k + 512], W[:, 256 * k:256 * k + 256].indirect(off), None, v_to, a_w)
-            v_low = tt(nl, lowv.indirect(off), lowc, A.min, v_to, v_low, v_lc)
-            lowv, lowc = nl, T["lc%d" % r][:, 256 * k:256 * k + 256]
-            if k < 7:
-                v_lc = act(lowc, lowv, None, v_low)
-                t = scan(sc(k + 1), m16, W[:, 256 * k + 256:256 * k + 512], a_w)
-                if r == 0:
-                    tables(k)
-                if k == 0:
-                    t4 = scan(SC[:, 9 * 256:9 * 256 + 128], m4[:, 0:128], W[:, 0:128])
-                if k == 1:
-                    ts(d1[:, 2:128:4], SC[:, 9 * 256 + 3:9 * 256 + 128:4], un4, tau4, A.mult, A.add, t4)
-                if k == 2:
-                    td = ts(d1[:, 130:160:4], SC[:, 15:128:16], un16, 1.0, A.mult, A.subtract)
-                if k == 3:
-                    td = ts(sm[:, 0:40], d1[:, 2:160:4], -2.0, None, A.mult, None, td)
-                if k == 4:
-                    v_d = tt(d0[:, 2:160:4], sm[:, 0:40], d1[:, 3:160:4], A.add, td)
-                v_to = ts(to[:, 16 * k + 16:16 * k + 32], SC[:, 256 * (k + 1) + 15:256 * (k + 2):16], un16, 1.0, A.mult, A.subtract, t)
+        lc = T["lc%d" % r]
+        v_low = vcopy(low[:, 128:256], W[:, 128:256], th)
+        v_lc = vcopy(lc[:, 128:256], W[:, 128:256])
+        a_w = act(W[:, 256:384], W[:, 0:256].indirect(to[:, 0:8]), None, v_tl)
+        v_w = vcopy(W[:, 384:512], W[:, 0:256].indirect(to[:, 8:16]), v_to)
+        scan(SC[:, 256:384], m16[:, 0:128], W[:, 256:384], a_w)
+        t = scan(SC[:, 384:512], m16[:, 0:128], W[:, 384:512], v_w)
+        t4 = scan(SC[:, 9 * 256:9 * 256 + 128], m4[:, 0:128], W[:, 0:128])
+        v_to = ts(to[:, 16:32], SC[:, 256 + 15:512:16], un16, 1.0, A.mult, A.subtract, t)
+        v_lc = (v_lc, a_pre[r])
+        for k in range(1, 7):
+            o, i, off = W[:, 256 * k + 256:256 * k + 512], W[:, 256 * k:256 * k + 256], to[:, 16 * k:16 * k + 16]
+            nl, pl = low[:, 256 * k:256 * k + 256], low[:, 256 * k - 256:256 * k]
+            if k < 6:
+                e = 256 - SHARE
+                a_w = act(o[:, 0:e], i.indirect(to[:, 16 * k:16 * k + e // 16]), None, v_to, a_w)
+                v_w = vcopy(o[:, e:256], i.indirect(to[:, 16 * k + e // 16:16 * k + 16]), v_to) if SHARE else None
+            else:
+                a_w = act(o[:, 128:256], i.indirect(to[:, 16 * k + 8:16 * k + 16]), None, v_to, a_w)
+            v_low = tt(nl, pl.indirect(off), lc[:, 256 * k - 256:256 * k], A.min, v_to, v_low, *v_lc)
+            if k < 6:
+                v_lc = (act(lc[:, 256 * k:256 * k + 256], nl, None, v_low),)
+                t = scan(sc(k + 1), m16, o, a_w, v_w)
+            else:
+                v_lc = (act(lc[:, 256 * k + 128:256 * k + 256], nl[:, 128:256], None, v_low),)
+                t = scan(SC[:, 256 * k + 384:256 * k + 512], m16[:, 0:128], o[:, 128:256], a_w)
+            if r == 0:
+                tables(k)
+            if k == 1:
+                ts(d1[:, 2:128:4], SC[:, 9 * 256 + 3:9 * 256 + 128:4], un4, tau4, A.mult, A.add, t4)
+            if k == 2:
+                td = ts(d1[:, 130:160:4], SC[:, 15:128:16], un16, 1.0, A.mult, A.subtract)
+            if k == 3:
+                td = ts(sm[:, 0:40], d1[:, 2:160:4], -2.0, None, A.mult, None, td)
+            if k == 4:
+                v_d = tt(d0[:, 2:160:4], sm[:, 0:40], d1[:, 3:160:4], A.add, td, tab[3])
+            h = 0 if k < 6 else 8
+            v_to = ts(to[:, 16 * k + 16 + h:16 * k + 32], SC[:, 256 * (k + 1) + 15 + 16 * h:256 * (k + 2):16], un16, 1.0, A.mult, A.subtract, t)
+        l8 = low[:, 7 * 256 + 128:8 * 256]
+        v_low = tt(l8, low[:, 6 * 256:7 * 256].indirect(to[:, 120:128]), lc[:, 6 * 256 + 128:7 * 256], A.min, v_to, v_low, *v_lc)
         so = T["so%d" % r]
-        t4 = scan(sc(10), m4, lowv, v_low)
-        t16 = scan(sc(11), m16, lowv)
-        tt(d1[:, 0:128:4], SC[:, 10 * 256 + 131:11 * 256:4], cmp4, A.is_equal, t4)
-        e4 = tt(d1[:, 1:128:4], SC[:, 10 * 256 + 3:10 * 256 + 128:4], cmp4, A.is_equal)
-        tt(d1[:, 128:160:4], SC[:, 11 * 256 + 143:12 * 256:16], cmp16, A.is_equal, t16)
-        e16 = tt(d1[:, 129:160:4], SC[:, 11 * 256 + 15:11 * 256 + 128:16], cmp16, A.is_equal)
+        scan(SC[:, 2560:2624], m2, l8[:, 0:64], v_low, tab[5])
+        t4 = scan(SC[:, 2624:2752], m4[:, 0:128], l8)
+        scan(SC[:, 2816:2880], m8, l8[:, 0:64])
+        t16 = scan(SC[:, 2880:3008], m16[:, 0:128], l8)
+        tt(d1[:, 1:128:4], SC[:, 2561:2624:2], cmp_[:, 40:72], A.is_equal, t4)
+        e4 = tt(d1[:, 0:128:4], SC[:, 2627:2752:4], cmp_[:, 0:32], A.is_equal)
+        tt(d1[:, 129:160:4], SC[:, 2823:2880:8], cmp_[:, 72:80], A.is_equal, t16)
+        e16 = tt(d1[:, 128:160:4], SC[:, 2895:3008:16], cmp_[:, 32:40], A.is_equal)
         s4 = chain(so[:, 0:128], d0[:, 0:128], d1[:, 0:128], e4, v_d)
         s16 = chain(so[:, 128:160], d0[:, 128:160], d1[:, 128:160], e16)
         clo = vcopy(tw[:, 0:32], so[:, 2:128:4], s4)
@@ -323,7 +376,8 @@ def rank_program(g, core, T, topo):
         z2 = tt(Z[:, 512:768], xk[:].indirect(tw[:, 40:56]), xk2[:, 512:768], A.add, chi)
         tq = quant(nm("qz")[:, 128:256], nm("qzs")[:, 128:256], Z[:, 256:768], z2)
         p = layer(nm("qz")[:, 128:256], nm("qzs")[:, 128:256], (4, 5, 6, 7), tq)
-        tq1 = quant(nm("qh")[:, 0:128], nm("qhs")[:, 0:128], H[:, 0:512], h1[3])
+        if not SINGLE:
+            tq1 = quant(nm("qh")[:, 0:128], nm("qhs")[:, 0:128], H[:, 0:512], h1[3])
         h2 = [None] * 4
         for b in (0, 2):
             h2[b] = ts(H[:, 512 + b:768:4], psv(4 + b, 64, 128), 0.03125, None, A.mult, None, p[b])
@@ -331,14 +385,20 @@ def rank_program(g, core, T, topo):
         for b in (1, 3):
             h2[b] = act(H[:, 512 + b:768:4], psv(4 + b, 64, 128), 0.03125, p[b])
             bankuse[4 + b] = [h2[b]]
-        tq2 = quant(nm("qh")[:, 128:256], nm("qhs")[:, 128:256], H[:, 256:768], h2[2], h2[3])
+        if SINGLE:
+            tq2 = quant(nm("qh")[:, 0:192], nm("qhs")[:, 0:192], H[:, 0:768], h1[3], h2[2], h2[3])
+            wait("g", tq2)
+            na = remote(r, nm("cin")[:, 0:192].bitcast(dt.uint8), nm("qh")[:, 0:192].bitcast(dt.uint8), "ra%d" % r)
+            na += remote(r, nm("cins")[:, 0:192], nm("qhs")[:, 0:192], "ra%d" % r)
+        else:
+            tq2 = quant(nm("qh")[:, 128:256], nm("qhs")[:, 128:256], H[:, 256:768], h2[2], h2[3])
 
-        wait("g", tq1)
-        na = remote(r, nm("cin")[:, 0:128].bitcast(dt.uint8), nm("qh")[:, 0:128].bitcast(dt.uint8), "ra%d" % r)
-        na += remote(r, nm("cins")[:, 0:128], nm("qhs")[:, 0:128], "ra%d" % r)
-        wait("g", tq2)
-        nb = remote(r, nm("cin")[:, 128:192].bitcast(dt.uint8), nm("qh")[:, 192:256].bitcast(dt.uint8), "rb%d" % r)
-        nb += remote(r, nm("cins")[:, 128:192], nm("qhs")[:, 192:256], "rb%d" % r)
+            wait("g", tq1)
+            na = remote(r, nm("cin")[:, 0:128].bitcast(dt.uint8), nm("qh")[:, 0:128].bitcast(dt.uint8), "ra%d" % r)
+            na += remote(r, nm("cins")[:, 0:128], nm("qhs")[:, 0:128], "ra%d" % r)
+            wait("g", tq2)
+            nb = remote(r, nm("cin")[:, 128:192].bitcast(dt.uint8), nm("qh")[:, 192:256].bitcast(dt.uint8), "rb%d" % r)
+            nb += remote(r, nm("cins")[:, 128:192], nm("qhs")[:, 192:256], "rb%d" % r)
 
         z3 = tt(Z[:, 768:1024], xk[:].indirect(tw[:, 56:72]), xk2[:, 768:1024], A.add)
         s16 = None
@@ -351,13 +411,15 @@ def rank_program(g, core, T, topo):
             t = act(B[:, 768 + b:1024:4], psv(b, 64, 128), 0.03125, p[b])
             bankuse[b] = [t]
         a_b = t
+        if not last:
+            prefill(r + 1)
         s4o = 256 * (13 if r else 9)
         if not last:
             kf = T["kf%d" % (r + 1)]
             v_k16 = ts(T["k16_%d" % (r + 1)][:], SC[:, 12 * 256 + 15:13 * 256:16], un16, 1.0, A.mult, A.subtract, s16)
             v_kf = ts(kf[:, 0:16], SC[:, 12 * 256 + 15:13 * 256:16], un16, 1.0, A.mult, A.subtract)
             v_k4 = ts(T["k4_%d" % (r + 1)][:], SC[:, s4o + 3:s4o + 256:4], un4, tau4, A.mult, A.add, s4)
-            t = tt(kf[:, 16:24], kf[:, 0:8], T.c127[:], A.max, v_kf)
+            t = tt(kf[:, 16:24], kf[:, 0:8], T.c127[:, 0:8], A.max, v_kf)
             v_kb = vcopy(T["kb%d" % (r + 1)][:], kf[:, 16:24], t)
             wait("g", v_k16)
             rk[r + 1] = remote(r + 1, T["kin%d" % (r + 1)][:], T["k16_%d" % (r + 1)][:], "rk%d" % (r + 1))
@@ -370,23 +432,32 @@ def rank_program(g, core, T, topo):
             v_v = quant(T.vq[:, 0:128], T.vqs[:, 0:128], T.vt[:], t_v)
 
         cin, cins = nm("cin"), nm("cins")
-        p = []
-        for b in range(4):
-            p.append(mm(4 + b, 128, T.eq[:, 128 * b:128 * b + 128], T.es[:, 128 * b:128 * b + 128], cin[:, 0:128], cins[:, 0:128],
-                        ("ra%d" % r, na), v_e, *bankuse[4 + b]))
-        for b in range(4):
-            t = act(B[:, b:512:4], psv(4 + b, 0, 128), None, p[b])
-            bankuse[4 + b] = [t]
-        p = []
-        for b in range(4):
-            p.append(mm(b, 128, T.eq[:, 128 * b:128 * b + 128], T.es[:, 128 * b:128 * b + 128], cin[:, 64:192], cins[:, 64:192],
-                        ("rb%d" % r, nb), *bankuse[b]))
-        bt = []
-        for b in range(4):
-            o, i = B[:, 512 + b:768:4], psv(b, 64, 128)
-            t = vcopy(o, i, p[b]) if b % 2 == 0 else act(o, i, None, p[b])
-            bankuse[b] = [t]
-            bt.append(t)
+        p, bt = [], []
+        if SINGLE:
+            for b in range(4):
+                p.append(mm(4 + b, 192, T.eq[:, 128 * b:128 * b + 128], T.es[:, 128 * b:128 * b + 128], cin[:, 0:192], cins[:, 0:192],
+                            ("ra%d" % r, na), v_e, *bankuse[4 + b]))
+            for b in range(4):
+                o, i = B[:, b:768:4], psv(4 + b, 0, 192)
+                t = vcopy(o, i, p[b]) if b % 2 == 0 else act(o, i, None, p[b])
+                bankuse[4 + b] = [t]
+                bt.append(t)
+        else:
+            for b in range(4):
+                p.append(mm(4 + b, 128, T.eq[:, 128 * b:128 * b + 128], T.es[:, 128 * b:128 * b + 128], cin[:, 0:128], cins[:, 0:128],
+                            ("ra%d" % r, na), v_e, *bankuse[4 + b]))
+            for b in range(4):
+                t = act(B[:, b:512:4], psv(4 + b, 0, 128), None, p[b])
+                bankuse[4 + b] = [t]
+            p = []
+            for b in range(4):
+                p.append(mm(b, 128, T.eq[:, 128 * b:128 * b + 128], T.es[:, 128 * b:128 * b + 128], cin[:, 64:192], cins[:, 64:192],
+                            ("rb%d" % r, nb), *bankuse[b]))
+            for b in range(4):
+                o, i = B[:, 512 + b:768:4], psv(b, 64, 128)
+                t = vcopy(o, i, p[b]) if b % 2 == 0 else act(o, i, None, p[b])
+                bankuse[b] = [t]
+                bt.append(t)
 
         nx, n4 = T["x%d" % (r + 1)], T["k4_%d" % (r + 1)]
         nq, ns = T["xq%d" % (r + 1)], T["xs%d" % (r + 1)]
@@ -413,6 +484,7 @@ def rank_program(g, core, T, topo):
     out("y", T.osc[4:8, :], xs[32:36, :])
     out("a", T.osc[8:12, :], xs[64:68, :])
     out("y", T.osc[12:16, :], xs[96:100, :])
-    out("a", T.y[:], T.yo[:], y1, y2)
+    out("y", T.y[:, 0:128], T.yo[:, 0:128], y1)
+    out("a", T.y[:, 128:256], T.yo[:, 128:256], y2)
 
     wait("g", ("dout", nd[0]), ("loc", loc[0]), *[(s, n) for s, n in done.items()])

from concourse.bass import DstId, RemoteDMATransfer
from concourse.mybir import dt, AluOpType, ActivationFunctionType

ROUNDS = 3
LIFT = 512.0
SINGLE = False
SHARE = 32
A = AluOpType
CP = ActivationFunctionType.Copy

SCRATCH = {
    "ps": ("psum", [128, 4096], "float32"),
    "kli": ("sbuf", [128, 16], "int32"),
    "ut": ("sbuf", [128, 512], "bfloat16"),
    "vt": ("sbuf", [128, 512], "bfloat16"),
    "uq": ("sbuf", [128, 128], "float8_e4m3fn_x4"), "us": ("sbuf", [128, 128], "uint8"),
    "up": ("sbuf", [128, 128], "float8_e4m3fn_x4"), "ups": ("sbuf", [128, 128], "uint8"),
    "vq": ("sbuf", [128, 128], "float8_e4m3fn_x4"), "vqs": ("sbuf", [128, 128], "uint8"),
    "wq": ("sbuf", [128, 512], "float8_e4m3fn_x4"), "wqs": ("sbuf", [128, 512], "uint8"),
    "ones": ("sbuf", [128, 512], "bfloat16"),
    "et": ("sbuf", [128, 2048], "bfloat16"),
    "eq": ("sbuf", [128, 512], "float8_e4m3fn_x4"), "es": ("sbuf", [128, 512], "uint8"),
    "pi": ("sbuf", [128, 8], "int32"),
    "cs": ("sbuf", [128, 24], "float32"),
    "i16": ("sbuf", [128, 16], "float32"), "ms": ("sbuf", [128, 64], "bfloat16"), "mw": ("sbuf", [128, 32], "bfloat16"),
    "oq": ("sbuf", [128, 16], "uint16"), "ot": ("sbuf", [128, 16], "uint16"),
    "mt": ("sbuf", [128, 512], "bfloat16"),
    "d0": ("sbuf", [128, 160], "float32"), "d1": ("sbuf", [128, 160], "float32"),
    "one": ("sbuf", [128, 256], "bfloat16"),
    "c21": ("sbuf", [128, 128], "bfloat16"), "c43": ("sbuf", [128, 128], "float32"),
    "ci": ("sbuf", [128, 40], "float32"), "cc": ("sbuf", [128, 120], "float32"),
    "cmp": ("sbuf", [128, 80], "float32"), "c127": ("sbuf", [128, 24], "float32"), "mk": ("sbuf", [128, 448], "bfloat16"),
    "uo": ("sbuf", [128, 8], "uint16"),
    "kyf": ("sbuf", [128, 256], "float32"),
    "yo": ("sbuf", [128, 256], "float32"),
    "x0": ("sbuf", [128, 1024], "bfloat16"),
}
for _r in range(ROUNDS + 1):
    if _r:
        SCRATCH["x%d" % _r] = ("sbuf", [128, 1024], "bfloat16")
    SCRATCH["xq%d" % _r] = ("sbuf", [128, 256], "float8_e4m3fn_x4")
    SCRATCH["xs%d" % _r] = ("sbuf", [128, 256], "uint8")
for _r in range(ROUNDS):
    for _n, _w, _d in (("xk", 1024, "bfloat16"), ("xj", 1024, "bfloat16"), ("lc", 8 * 256, "bfloat16"), ("z", 1024, "bfloat16"), ("h", 768, "bfloat16"), ("b", 1024, "bfloat16"),
                       ("bit", 272, "bfloat16"), ("w", 8 * 256, "bfloat16"), ("low", 8 * 256, "bfloat16"),
                       ("sc", 14 * 256, "bfloat16"), ("fr", 4 * 256, "bfloat16"), ("sm", 48, "float32"), ("so", 160, "float32"),
                       ("to", 8 * 16, "uint16"), ("tt", 80, "uint16"),
                       ("kf", 24, "float32"), ("k16_", 16, "uint16"), ("kb", 8, "uint16"), ("k4_", 64, "uint16"),
                       ("kin", 16, "uint16")):
        SCRATCH["%s%d" % (_n, _r)] = ("sbuf", [128, _w], _d)
    for _n, _w in (("qz", 384), ("qh", 256), ("cin", 192)):
        SCRATCH["%s_%d" % (_n, _r)] = ("sbuf", [128, _w], "float8_e4m3fn_x4")
        SCRATCH["%ss_%d" % (_n, _r)] = ("sbuf", [128, _w], "uint8")
SCRATCH["k4_3"] = ("sbuf", [128, 64], "uint16")

SEMAPHORES = ["sv", "sa", "st", "sg", "dx", "du", "dk", "dwc", "dws", "dv", "dxk", "dout", "loc"]
SEMAPHORES += ["%s%d" % (n, r) for r in range(ROUNDS) for n in ("rk", "ra", "rb")]


def rank_program(g, core, T, topo):
    rank = T.rank_of(core)
    if rank is None:
        return
    queues = {"v": g.vector, "a": g.scalar, "t": g.tensor, "g": g, "y": g.sync}
    own = {"v": "sv", "a": "sa", "t": "st", "g": "sg"}
    done = {"sv": 0, "sa": 0, "st": 0, "sg": 0}
    seen = {q: {} for q in queues}

    def wait(q, *toks):
        need = {}
        for t in toks:
            if t is not None:
                need[t[0]] = max(need.get(t[0], 0), t[1])
        for s, n in need.items():
            if seen[q].get(s, 0) < n:
                queues[q].wait_ge(T.sem[s], n)
                seen[q][s] = n

    def fin(q, ins):
        s = own[q]
        ins.then_inc(T.sem[s], 1)
        done[s] += 1
        return (s, done[s])

    def dma(q, sem, total, out, in_):
        queues[q].dma_start(out, in_).then_inc(T.sem[sem], 16)
        return (sem, total)

    def ts(out, in0, s1, s2, op0, op1, *toks):
        wait("v", *toks)
        if op1 is None:
            return fin("v", g.vector.tensor_scalar(out, in0, s1, None, op0))
        return fin("v", g.vector.tensor_scalar(out, in0, s1, s2, op0, op1))

    def tt(out, in0, in1, op, *toks):
        wait("v", *toks)
        return fin("v", g.vector.tensor_tensor(out, in0, in1, op))

    def vcopy(out, in_, *toks):
        wait("v", *toks)
        return fin("v", g.vector.tensor_copy(out, in_))

    def scan(out, mask, data, *toks):
        wait("v", *toks)
        return fin("v", g.vector.tensor_tensor_scan(out, mask, data, 0.0, A.mult, A.max))

    def chain(out, mul, add, *toks):
        wait("v", *toks)
        return fin("v", g.vector.tensor_tensor_scan(out, mul, add, 0.0, A.mult, A.add))

    def quant(codes, plane, tile, *toks):
        wait("v", *toks)
        return fin("v", g.vector.quantize_mx(codes, plane, tile))

    def act(out, in_, scale, *toks):
        wait("a", *toks)
        if scale is None:
            return fin("a", g.scalar.activation(out, in_, CP))
        return fin("a", g.scalar.activation(out, in_, CP, scale=scale))

    def mm(bank, n, lq, ls, rq, rs, *toks):
        wait("t", *toks)
        return fin("t", g.tensor.matmul_mx(T.ps[:, 512 * bank:512 * bank + n], lq, ls, rq, rs, True, True))

    def psv(bank, a, b):
        return T.ps[:, 512 * bank + a:512 * bank + b]

    def remote(r, out, in_, sem):
        dst = T.cores[rank ^ (1 << r)]
        rid, pid, _ = topo.addr(dst)
        ne = len(topo.engines(core, dst))
        g.remote_dma(out, in_, T.sem[sem], T.sem.loc, pid, rid, topo.mask(core, dst))
        loc[0] += ne
        return ne

    loc = [0]
    cs, d0, d1 = T.cs, T.d0, T.d1

    t_kl = dma("y", "dk", 16, T.kli[:], T.kl[:])
    t_x = dma("y", "dx", 16, T.x0[:], T.x[:])
    t_u = dma("a", "du", 16, T.ut[:], T.u[:])
    t_wc = dma("y", "dwc", 16, T.wq[:, 0:512].bitcast(dt.uint8), T.wc[:])
    t_ws = dma("y", "dws", 16, T.wqs[:], T.ws[:])
    t_v = dma("y", "dv", 16, T.vt[:], T.v[:])

    def iota(out, pat, base, ch, small=True):
        if small:
            return fin("g", g.iota(out, pat, base, ch, allow_small_or_imprecise_dtypes=True))
        return fin("g", g.iota(out, pat, base, ch))
    g_pi = iota(T.pi[:, 0:1], [[0, 1]], 0, 1, False)
    g_is = iota(T.i16[:], [[1, 16]], 0, 0)
    g_ci = iota(T.ci[:, 32:40], [[16, 8]], 0, 0)
    g_ci4 = iota(T.ci[:, 0:32], [[4, 32]], 0, 0)
    g_one = iota(T.one[:], [[1, 256]], 1, 0)
    g_c21 = iota(T.c21[:], [[2, 128]], 1, 0)
    g_c43 = iota(T.c43[:], [[4, 128]], 3, 0)
    g_i2 = iota(T.mk[:, 0:64], [[0, 32], [1, 2]], 0, 0)
    g_i8 = iota(T.mk[:, 64:128], [[0, 8], [1, 8]], 0, 0)
    a_pre = [None] * ROUNDS

    def prefill(r):
        act(T["low%d" % r][:, 0:128], T.one[:, 0:128], None, g_one)
        a_pre[r] = act(T["lc%d" % r][:, 0:128], T.one[:, 0:128], None)

    v_bit = fin("v", g.vector.memset(T.bit0[:, 256:272], 1.0))
    ts(T.pi[:, 1:2], T.pi[:, 0:1], 15, None, A.bitwise_and, None, g_pi)
    ts(T.pi[:, 2:3], T.pi[:, 0:1], 2, 3, A.logical_shift_right, A.bitwise_and)
    ts(T.pi[:, 4:5], T.pi[:, 0:1], 1, 7, A.logical_shift_right, A.bitwise_and)
    t = ts(T.pi[:, 3:4], T.pi[:, 0:1], 3, None, A.bitwise_and, None)
    v_uo = vcopy(T.uo[:], T.ci[:, 32:40], g_ci)
    vcopy(cs[:, 15:16], T.pi[:, 4:5], t)
    t = vcopy(cs[:, 0:3], T.pi[:, 1:4])
    q_, r_ = cs[:, 0:1], cs[:, 1:2]

    def fun(f, out, in_, scale, bias, *toks):
        wait("a", *toks)
        return fin("a", g.scalar.activation(out, in_, f, bias=bias, scale=scale))
    ID, SG = ActivationFunctionType.Identity, ActivationFunctionType.Sign
    fun(SG, cs[:, 8:9], q_, 1.0, -14.5, t)
    a_cs = fun(SG, cs[:, 20:21], r_, 1.0, -2.5)
    h = LIFT / 2
    fun(ID, cs[:, 4:5], cs[:, 8:9], 0.5 - 0.5 / LIFT, 0.5 + 0.5 / LIFT, a_cs)
    fun(ID, cs[:, 5:6], cs[:, 20:21], 2.0 - 2.0 / LIFT, 2.0 + 2.0 / LIFT)
    fun(ID, cs[:, 6:7], cs[:, 8:9], 0.5 - h, 0.5 + h)
    a_cs = fun(ID, cs[:, 7:8], cs[:, 20:21], 0.5 - h, 0.5 + h)
    prefill(0)
    ms, mw = T.ms, T.mw
    ts(ms[:, 16:32], T.i16[:], q_, 1.0, A.subtract, A.is_equal, g_is, t)
    ta = ts(ms[:, 36:40], T.i16[:, 0:4], r_, 1.0, A.subtract, A.is_equal)
    ts(ms[:, 0:16], T.i16[:], q_, 0.0, A.subtract, A.is_gt)
    ts(ms[:, 32:36], T.i16[:, 0:4], r_, 0.0, A.subtract, A.is_gt)
    ts(ms[:, 40:56], ms[:, 16:32], LIFT, None, A.mult, None, ta)
    tb = ts(ms[:, 56:60], ms[:, 36:40], LIFT, None, A.mult, None)
    ts(T.oq[:], T.i16[:], 0.0, q_, A.mult, A.add)
    ts(T.ot[:], T.i16[:], 0.0, cs[:, 2:3], A.mult, A.add)
    tt(mw[:, 0:16], ms[:, 0:16], ms[:, 40:56], A.max, tb)
    t = tt(mw[:, 16:20], ms[:, 32:36], ms[:, 56:60], A.max)
    m16, m4 = T.mt[:, 0:256], T.mt[:, 256:512]
    act(m16, mw[:, 0:16].indirect(T.oq[:]), None, t)
    a_m = act(m4, mw[:, 16:20].indirect(T.ot[:]), None)

    v_t4 = ts(cs[:, 3:4], cs[:, 2:3], 4.0, None, A.subtract, None)
    v_cs = a_cs
    un16, un4, tau4 = cs[:, 4:5], cs[:, 5:6], cs[:, 3:4]

    cc = T.cc
    v_cc = ts(cc[:, 32:40], T.ci[:, 32:40], q_, None, A.add, None)
    t = ts(T.c127[:, 8:16], cc[:, 32:40], 4.0, 3.0, A.mult, A.add, v_cc)
    v_c127 = ts(T.c127[:, 0:8], cc[:, 32:40], 127.0, 256.0, A.is_equal, A.mult)
    v_hic = ts(T.c127[:, 16:24], T.c127[:, 8:16], cs[:, 6:7], None, A.mult, None, t, a_cs)

    def tables(k):
        h = LIFT / 2
        if k == 1:
            tab[1] = fun(ID, cs[:, 12:13], tau4, 2.0, 12.0, v_t4)
            fin("v", g.vector.memset(d0[:], -1.0))
            tab["bit"] = [None] + [fin("v", g.vector.memset(T["bit%d" % i][:, 256:272], 1.0)) for i in (1, 2)]
        if k == 2:
            fun(ID, cs[:, 13:14], cs[:, 18:19], 0.5 - h, 0.5 + h, tab[1])
            fun(ID, cs[:, 14:15], cs[:, 19:20], 0.5 - h, 0.5 + h)
            tab["sg"] = fun(SG, cc[:, 40:80], cc[:, 0:40], 1.0, -0.5, v_c127)
            ts(d0[:, 0:160:4], d0[:, 0:160:4], 0.0, None, A.mult, None)
            fun(ID, cs[:, 11:12], cs[:, 18:19], -h, h)
            fun(SG, mk[:, 256:320], mk[:, 64:128], 1.0, cs[:, 16:17], g_i8)
            tab[2] = fun(ActivationFunctionType.Abs, mk[:, 320:384], mk[:, 64:128], 1.0, cs[:, 17:18])
        if k == 3:
            fun(ID, d1[:, 3:128:4], cc[:, 0:32], 16.0, cs[:, 12:13], tab[2])
            fun(ID, d1[:, 131:160:4], cc[:, 32:40], 4.0, 1.0)
            fun(ActivationFunctionType.Relu, mk[:, 384:448], mk[:, 320:384], -LIFT, LIFT)
            tab[3] = fun(ID, mk[:, 128:192], mk[:, 0:64], cs[:, 11:12], 0.0, g_i2)
            tab["cy"] = tt(cc[:, 80:120], cc[:, 0:40], cc[:, 40:80], A.add, tab["sg"])
        if k == 5:
            fun(ID, cmp_[:, 0:32], cc[:, 80:112], cs[:, 7:8], 0.0, tab["cy"])
            fun(ID, cmp_[:, 32:40], cc[:, 112:120], cs[:, 6:7], 0.0)
            fun(ID, cmp_[:, 40:72], cc[:, 80:112], cs[:, 13:14], 0.0)
            tab[5] = fun(ID, cmp_[:, 72:80], cc[:, 112:120], cs[:, 14:15], 0.0)
            tab["m8"] = tt(mk[:, 192:256], mk[:, 256:320], mk[:, 384:448], A.max, tab[3])
    tab = {}

    cmp_, mk, hic = T.cmp, T.mk, T.c127[:, 16:24]
    m2, m8 = mk[:, 128:192], mk[:, 192:256]

    v_k16 = vcopy(T.k16_0[:], T.kli[:], t_kl)
    v_kf = vcopy(T.kf0[:, 0:16], T.kli[:])

    v_uq = quant(T.uq[:, 0:128], T.us[:, 0:128], T.ut[:, 0:512], t_u)
    tk = tt(T.kf0[:, 16:24], T.kf0[:, 0:8], T.c127[:, 0:8], A.max, v_kf, v_c127)
    v_up = vcopy(T.up[:, 0:128].bitcast(dt.uint32), T.uq[:, 0:128].bitcast(dt.uint32).indirect(T.uo[:, 0:8]), v_uq, v_uo)
    v_kb = vcopy(T.kb0[:], T.kf0[:, 16:24], tk)
    v_q1 = quant(T.xq0[:, 0:128], T.xs0[:, 0:128], T.x0[:, 0:512], t_x)
    a_up = act(T.ups[:, 0:128], T.us[:, 0:128].indirect(T.uo[:, 0:8]), None, v_uq, v_uo)
    a_kfr = act(T.fr0[:, 0:256], T.one[:].indirect(T.k16_0[:, 0:16]), None, v_k16, g_one)
    fun(SG, cs[:, 18:19], r_, 1.0, -1.5)
    fun(SG, cs[:, 19:20], q_, 1.0, -13.5)
    fun(ID, cc[:, 0:32], T.ci[:, 0:32], 1.0, r_, g_ci4)
    fun(ID, cs[:, 16:17], cs[:, 15:16], -1.0, 0.0)
    fun(ID, cs[:, 17:18], cs[:, 15:16], -1.0, -1.0)
    v_q2 = quant(T.xq0[:, 128:256], T.xs0[:, 128:256], T.x0[:, 512:1024])
    t = scan(T.sc0[:, 13 * 256:14 * 256], m4, T.fr0[:, 0:256], a_kfr, a_m)
    v_k4 = ts(T.k4_0[:], T.sc0[:, 13 * 256 + 3:14 * 256:4], un4, tau4, A.mult, A.add, t, v_cs)

    wait("g", v_k16)
    rk = [remote(0, T.kin0[:], T.k16_0[:], "rk0"), 0, 0]
    g_e = []
    wait("g", iota(T.ones[:], [[0, 512]], 1, 0))
    for b in range(4):
        g_e.append(fin("g", g.affine_select(T.et[:, 512 * b:512 * b + 512], T.ones[:], [[-1, 512]], A.is_equal, 0.0, b, 4)))

    bankuse = [[] for _ in range(8)]
    x_done = (t_x,)
    for r in range(ROUNDS):
        X, xk, Z, H, B = T["x%d" % r], T["xk%d" % r], T["z%d" % r], T["h%d" % r], T["b%d" % r]
        xq, xs, bit, W, low, SC = T["xq%d" % r], T["xs%d" % r], T["bit%d" % r], T["w%d" % r], T["low%d" % r], T["sc%d" % r]
        fr, sm, to, tw = T["fr%d" % r], T["sm%d" % r], T["to%d" % r], T["tt%d" % r]
        last = r == ROUNDS - 1

        def sc(i):
            return SC[:, 256 * i:256 * i + 256]

        a_xk = act(xk[:], X[:].indirect(T["k4_%d" % r][:, 0:64]), 0.5, v_k4, *x_done)
        xk2 = T["xj%d" % r]
        wait("y", a_xk)
        d_xk = dma("y", "dxk", 16 * (r + 1), xk2[:], xk[:])

        sb = (4, 5)
        p1 = mm(sb[0], 128, T.up[:, 0:128], T.ups[:, 0:128], xq[:, 0:128], xs[:, 0:128], v_q1, v_up, a_up, *bankuse[sb[0]])
        p2 = mm(sb[1], 128, T.up[:, 0:128], T.ups[:, 0:128], xq[:, 128:256], xs[:, 128:256], v_q2, *bankuse[sb[1]])
        ts(bit[:, 0:128], psv(sb[0], 0, 128), 0.0, None, A.is_gt, None, p1)
        t = ts(bit[:, 128:256], psv(sb[1], 0, 128), 0.0, None, A.is_gt, None, p2)
        bankuse[sb[0]], bankuse[sb[1]] = [t], [t]
        tl = tt(W[:, 0:128], bit[:, 0:272].indirect(T["kb%d" % r][:, 0:8]), T.c21[:], A.add, t, v_kb, tab["bit"][r] if r else v_bit, g_c21)
        t = scan(SC[:, 0:128], m16[:, 0:128], W[:, 0:128], tl)
        th = tt(W[:, 128:256], T.c43[:], W[:, 0:128], A.subtract, g_c43)
        t = tt(sm[:, 40:48], hic, SC[:, 15:128:16], A.subtract, t, v_hic)
        v_tl = ts(to[:, 0:8], SC[:, 15:128:16], un16, 1.0, A.mult, A.subtract)
        v_to = ts(to[:, 8:16], sm[:, 40:48], un16, 1.0, A.mult, A.subtract, t)

        lc = T["lc%d" % r]
        v_low = vcopy(low[:, 128:256], W[:, 128:256], th)
        v_lc = vcopy(lc[:, 128:256], W[:, 128:256])
        a_w = act(W[:, 256:384], W[:, 0:256].indirect(to[:, 0:8]), None, v_tl)
        v_w = vcopy(W[:, 384:512], W[:, 0:256].indirect(to[:, 8:16]), v_to)
        scan(SC[:, 256:384], m16[:, 0:128], W[:, 256:384], a_w)
        t = scan(SC[:, 384:512], m16[:, 0:128], W[:, 384:512], v_w)
        t4 = scan(SC[:, 9 * 256:9 * 256 + 128], m4[:, 0:128], W[:, 0:128])
        v_to = ts(to[:, 16:32], SC[:, 256 + 15:512:16], un16, 1.0, A.mult, A.subtract, t)
        v_lc = (v_lc, a_pre[r])
        for k in range(1, 7):
            o, i, off = W[:, 256 * k + 256:256 * k + 512], W[:, 256 * k:256 * k + 256], to[:, 16 * k:16 * k + 16]
            nl, pl = low[:, 256 * k:256 * k + 256], low[:, 256 * k - 256:256 * k]
            if k < 6:
                e = 256 - SHARE
                a_w = act(o[:, 0:e], i.indirect(to[:, 16 * k:16 * k + e // 16]), None, v_to, a_w)
                v_w = vcopy(o[:, e:256], i.indirect(to[:, 16 * k + e // 16:16 * k + 16]), v_to) if SHARE else None
            else:
                a_w = act(o[:, 128:256], i.indirect(to[:, 16 * k + 8:16 * k + 16]), None, v_to, a_w)
            v_low = tt(nl, pl.indirect(off), lc[:, 256 * k - 256:256 * k], A.min, v_to, v_low, *v_lc)
            if k < 6:
                v_lc = (act(lc[:, 256 * k:256 * k + 256], nl, None, v_low),)
                t = scan(sc(k + 1), m16, o, a_w, v_w)
            else:
                v_lc = (act(lc[:, 256 * k + 128:256 * k + 256], nl[:, 128:256], None, v_low),)
                t = scan(SC[:, 256 * k + 384:256 * k + 512], m16[:, 0:128], o[:, 128:256], a_w)
            if r == 0:
                tables(k)
            if k == 1:
                ts(d1[:, 2:128:4], SC[:, 9 * 256 + 3:9 * 256 + 128:4], un4, tau4, A.mult, A.add, t4)
            if k == 2:
                td = ts(d1[:, 130:160:4], SC[:, 15:128:16], un16, 1.0, A.mult, A.subtract)
            if k == 3:
                td = ts(sm[:, 0:40], d1[:, 2:160:4], -2.0, None, A.mult, None, td)
            if k == 4:
                v_d = tt(d0[:, 2:160:4], sm[:, 0:40], d1[:, 3:160:4], A.add, td, tab[3])
            h = 0 if k < 6 else 8
            v_to = ts(to[:, 16 * k + 16 + h:16 * k + 32], SC[:, 256 * (k + 1) + 15 + 16 * h:256 * (k + 2):16], un16, 1.0, A.mult, A.subtract, t)
        l8 = low[:, 7 * 256 + 128:8 * 256]
        v_low = tt(l8, low[:, 6 * 256:7 * 256].indirect(to[:, 120:128]), lc[:, 6 * 256 + 128:7 * 256], A.min, v_to, v_low, *v_lc)
        so = T["so%d" % r]
        scan(SC[:, 2560:2624], m2, l8[:, 0:64], v_low, tab[5])
        t4 = scan(SC[:, 2624:2752], m4[:, 0:128], l8)
        scan(SC[:, 2816:2880], m8, l8[:, 0:64])
        t16 = scan(SC[:, 2880:3008], m16[:, 0:128], l8)
        tt(d1[:, 1:128:4], SC[:, 2561:2624:2], cmp_[:, 40:72], A.is_equal, t4)
        e4 = tt(d1[:, 0:128:4], SC[:, 2627:2752:4], cmp_[:, 0:32], A.is_equal)
        tt(d1[:, 129:160:4], SC[:, 2823:2880:8], cmp_[:, 72:80], A.is_equal, t16)
        e16 = tt(d1[:, 128:160:4], SC[:, 2895:3008:16], cmp_[:, 32:40], A.is_equal)
        s4 = chain(so[:, 0:128], d0[:, 0:128], d1[:, 0:128], e4, v_d)
        s16 = chain(so[:, 128:160], d0[:, 128:160], d1[:, 128:160], e16)
        clo = vcopy(tw[:, 0:32], so[:, 2:128:4], s4)
        chi = vcopy(tw[:, 40:72], so[:, 3:128:4])
        c16 = vcopy(tw[:, 32:40], so[:, 130:160:4], s16)

        ne = rk[r]
        f1 = act(fr[:, 256:512], T.one[:].indirect(T["kin%d" % r][:, 0:16]), None, ("rk%d" % r, ne), g_one)
        f2 = act(fr[:, 512:768], fr[:, 256:512].indirect(T["k16_%d" % r][:, 0:16]), None, f1, v_k16)
        act(fr[:, 768:896], fr[:, 512:768].indirect(tw[:, 32:40]), None, f2, c16)

        def layer(qz, qzs, banks, tok):
            out = []
            for b in range(4):
                out.append(mm(banks[b], 128, T.wq[:, 128 * b:128 * b + 128], T.wqs[:, 128 * b:128 * b + 128], qz, qzs,
                              tok, t_wc, t_ws, *bankuse[banks[b]]))
            return out

        def nm(s):
            return T["%s_%d" % (s, r)]
        z1 = tt(Z[:, 0:512], xk[:].indirect(tw[:, 0:32]), xk2[:, 0:512], A.add, clo, a_xk, d_xk)
        chi16 = vcopy(tw[:, 72:80], so[:, 131:160:4])
        a_n = act(fr[:, 896:1024], fr[:, 512:768].indirect(tw[:, 72:80]), None, chi16)
        tq = quant(nm("qz")[:, 0:128], nm("qzs")[:, 0:128], Z[:, 0:512], z1)
        p = layer(nm("qz")[:, 0:128], nm("qzs")[:, 0:128], (0, 1, 2, 3), tq)
        h1 = []
        for b in range(4):
            h1.append(act(H[:, b:512:4], psv(b, 0, 128), 0.03125, p[b]))
            bankuse[b] = [h1[b]]
        z2 = tt(Z[:, 512:768], xk[:].indirect(tw[:, 40:56]), xk2[:, 512:768], A.add, chi)
        tq = quant(nm("qz")[:, 128:256], nm("qzs")[:, 128:256], Z[:, 256:768], z2)
        p = layer(nm("qz")[:, 128:256], nm("qzs")[:, 128:256], (4, 5, 6, 7), tq)
        if not SINGLE:
            tq1 = quant(nm("qh")[:, 0:128], nm("qhs")[:, 0:128], H[:, 0:512], h1[3])
        h2 = [None] * 4
        for b in (0, 2):
            h2[b] = ts(H[:, 512 + b:768:4], psv(4 + b, 64, 128), 0.03125, None, A.mult, None, p[b])
            bankuse[4 + b] = [h2[b]]
        for b in (1, 3):
            h2[b] = act(H[:, 512 + b:768:4], psv(4 + b, 64, 128), 0.03125, p[b])
            bankuse[4 + b] = [h2[b]]
        if SINGLE:
            tq2 = quant(nm("qh")[:, 0:192], nm("qhs")[:, 0:192], H[:, 0:768], h1[3], h2[2], h2[3])
            wait("g", tq2)
            na = remote(r, nm("cin")[:, 0:192].bitcast(dt.uint8), nm("qh")[:, 0:192].bitcast(dt.uint8), "ra%d" % r)
            na += remote(r, nm("cins")[:, 0:192], nm("qhs")[:, 0:192], "ra%d" % r)
        else:
            tq2 = quant(nm("qh")[:, 128:256], nm("qhs")[:, 128:256], H[:, 256:768], h2[2], h2[3])

            wait("g", tq1)
            na = remote(r, nm("cin")[:, 0:128].bitcast(dt.uint8), nm("qh")[:, 0:128].bitcast(dt.uint8), "ra%d" % r)
            na += remote(r, nm("cins")[:, 0:128], nm("qhs")[:, 0:128], "ra%d" % r)
            wait("g", tq2)
            nb = remote(r, nm("cin")[:, 128:192].bitcast(dt.uint8), nm("qh")[:, 192:256].bitcast(dt.uint8), "rb%d" % r)
            nb += remote(r, nm("cins")[:, 128:192], nm("qhs")[:, 192:256], "rb%d" % r)

        z3 = tt(Z[:, 768:1024], xk[:].indirect(tw[:, 56:72]), xk2[:, 768:1024], A.add)
        s16 = None
        if not last:
            s16 = scan(sc(12), m16, fr[:, 768:1024], a_n)
        s4 = scan(sc(13) if r else sc(9), m4, fr[:, 768:1024], a_n)
        tq = quant(nm("qz")[:, 256:384], nm("qzs")[:, 256:384], Z[:, 512:1024], z3)
        p = layer(nm("qz")[:, 256:384], nm("qzs")[:, 256:384], (0, 1, 2, 3), tq)
        for b in range(4):
            t = act(B[:, 768 + b:1024:4], psv(b, 64, 128), 0.03125, p[b])
            bankuse[b] = [t]
        a_b = t
        if not last:
            prefill(r + 1)
        s4o = 256 * (13 if r else 9)
        if not last:
            kf = T["kf%d" % (r + 1)]
            v_k16 = ts(T["k16_%d" % (r + 1)][:], SC[:, 12 * 256 + 15:13 * 256:16], un16, 1.0, A.mult, A.subtract, s16)
            v_kf = ts(kf[:, 0:16], SC[:, 12 * 256 + 15:13 * 256:16], un16, 1.0, A.mult, A.subtract)
            v_k4 = ts(T["k4_%d" % (r + 1)][:], SC[:, s4o + 3:s4o + 256:4], un4, tau4, A.mult, A.add, s4)
            t = tt(kf[:, 16:24], kf[:, 0:8], T.c127[:, 0:8], A.max, v_kf)
            v_kb = vcopy(T["kb%d" % (r + 1)][:], kf[:, 16:24], t)
            wait("g", v_k16)
            rk[r + 1] = remote(r + 1, T["kin%d" % (r + 1)][:], T["k16_%d" % (r + 1)][:], "rk%d" % (r + 1))
        else:
            v_k4 = ts(T["k4_%d" % (r + 1)][:], SC[:, s4o + 3:s4o + 256:4], un4, tau4, A.mult, A.add, s4)
            v_ky = ts(T.kyf[:], fr[:, 768:1024], 1.0, None, A.subtract, None)
        if r == 0:
            for b in range(4):
                v_e = quant(T.eq[:, 128 * b:128 * b + 128], T.es[:, 128 * b:128 * b + 128], T.et[:, 512 * b:512 * b + 512], g_e[b])
            v_v = quant(T.vq[:, 0:128], T.vqs[:, 0:128], T.vt[:], t_v)

        cin, cins = nm("cin"), nm("cins")
        p, bt = [], []
        if SINGLE:
            for b in range(4):
                p.append(mm(4 + b, 192, T.eq[:, 128 * b:128 * b + 128], T.es[:, 128 * b:128 * b + 128], cin[:, 0:192], cins[:, 0:192],
                            ("ra%d" % r, na), v_e, *bankuse[4 + b]))
            for b in range(4):
                o, i = B[:, b:768:4], psv(4 + b, 0, 192)
                t = vcopy(o, i, p[b]) if b % 2 == 0 else act(o, i, None, p[b])
                bankuse[4 + b] = [t]
                bt.append(t)
        else:
            for b in range(4):
                p.append(mm(4 + b, 128, T.eq[:, 128 * b:128 * b + 128], T.es[:, 128 * b:128 * b + 128], cin[:, 0:128], cins[:, 0:128],
                            ("ra%d" % r, na), v_e, *bankuse[4 + b]))
            for b in range(4):
                t = act(B[:, b:512:4], psv(4 + b, 0, 128), None, p[b])
                bankuse[4 + b] = [t]
            p = []
            for b in range(4):
                p.append(mm(b, 128, T.eq[:, 128 * b:128 * b + 128], T.es[:, 128 * b:128 * b + 128], cin[:, 64:192], cins[:, 64:192],
                            ("rb%d" % r, nb), *bankuse[b]))
            for b in range(4):
                o, i = B[:, 512 + b:768:4], psv(b, 64, 128)
                t = vcopy(o, i, p[b]) if b % 2 == 0 else act(o, i, None, p[b])
                bankuse[b] = [t]
                bt.append(t)

        nx, n4 = T["x%d" % (r + 1)], T["k4_%d" % (r + 1)]
        nq, ns = T["xq%d" % (r + 1)], T["xs%d" % (r + 1)]
        g1 = tt(nx[:, 0:512], B[:].indirect(n4[:, 0:32]), X[:, 0:512], A.add, v_k4, a_b, *bt)
        g2 = tt(nx[:, 512:1024], B[:].indirect(n4[:, 32:64]), X[:, 512:1024], A.add)
        v_q1 = quant(nq[:, 0:128], ns[:, 0:128], nx[:, 0:512], g1)
        v_q2 = quant(nq[:, 128:256], ns[:, 128:256], nx[:, 512:1024], g2)
        x_done = (g1, g2)

    nd = [0]

    def out(q, o, i, *toks):
        wait(q, *toks)
        queues[q].dma_start(o, i).then_inc(T.sem.dout, 16)
        nd[0] += 16
    xq, xs = T["xq%d" % ROUNDS], T["xs%d" % ROUNDS]
    p1 = mm(4, 128, T.vq[:, 0:128], T.vqs[:, 0:128], xq[:, 0:128], xs[:, 0:128], v_q1, v_v, *bankuse[4])
    p2 = mm(5, 128, T.vq[:, 0:128], T.vqs[:, 0:128], xq[:, 128:256], xs[:, 128:256], v_q2, *bankuse[5])
    y1 = vcopy(T.yo[:, 0:128], psv(4, 0, 128), p1)
    y2 = vcopy(T.yo[:, 128:256], psv(5, 0, 128), p2)
    out("y", T.kp[:], T.kyf[0:128:16, :], v_ky)
    out("y", T.oc[:], xq[:, 0:256].bitcast(dt.uint8), v_q2)
    out("a", T.osc[0:4, :], xs[0:4, :], v_q2)
    out("y", T.osc[4:8, :], xs[32:36, :])
    out("a", T.osc[8:12, :], xs[64:68, :])
    out("y", T.osc[12:16, :], xs[96:100, :])
    out("y", T.y[:, 0:128], T.yo[:, 0:128], y1)
    out("a", T.y[:, 128:256], T.yo[:, 128:256], y2)

    wait("g", ("dout", nd[0]), ("loc", loc[0]), *[(s, n) for s, n in done.items()])
